import numpy as np
import ml_dtypes


def mxq(x, axis, fmt="e4m3"):
    dtype, down = {"e4m3": (ml_dtypes.float8_e4m3fn, 7), "e5m2": (ml_dtypes.float8_e5m2, 14)}[fmt]
    v = np.moveaxis(np.asarray(x, np.float32).astype(ml_dtypes.bfloat16).astype(np.float64), axis, -1)
    blocks = v.reshape(v.shape[:-1] + (-1, 32))
    amax = np.abs(blocks).max(-1, keepdims=True)
    byte = np.maximum(np.where(amax > 0, np.frexp(amax)[1] - 1 + 127, 0) - down, 1)
    scale = np.exp2(byte - 127.0)
    codes = (blocks / scale).astype(np.float32).astype(dtype).astype(np.float64)
    return np.moveaxis((codes * scale).reshape(v.shape), -1, axis)


WIDE = False


def mx_kscale(k):
    if not WIDE:
        return np.ones(k)
    levels = np.array([10, -10, 5, -5, 0])
    if k % 512:
        return np.exp2(np.random.permutation(np.resize(levels, k // 32))).repeat(32)
    a = np.empty((k // 512, 16))
    for p in range(k // 512):
        a[p, :8] = np.random.permutation(np.resize(levels, 8))
        for g in range(8):
            far = levels[np.abs(levels - a[p, g]) >= 10]
            a[p, g + 8] = far[np.random.randint(len(far))]
    return np.exp2(a.ravel()).repeat(32)


def f64(x):
    return np.asarray(x).astype(np.float64)


def striped(idx):
    return np.tile(idx.reshape(-1, 16).T, (8, 1)).astype(np.uint16)


def unstriped(offs):
    return offs[:16].T.reshape(-1).astype(np.int64)


E2M1 = np.array([0.0, 0.5, 1.0, 1.5, 2.0, 3.0, 4.0, 6.0, -0.0, -0.5, -1.0, -1.5, -2.0, -3.0, -4.0, -6.0])


def pack_weight(w, fmt):
    k, n = w.shape
    w = f64(np.asarray(w, np.float32).astype(ml_dtypes.bfloat16)).reshape(k // 32, 32, n)
    amax = np.abs(w).max(1)
    if fmt == "e4m3":
        byte = np.frexp(amax)[1] - 1 + 127 - 7
    else:
        mant, ex = np.frexp(amax / 6.0)
        byte = np.where(mant > 0.5, ex, ex - 1) + 127
    byte = np.clip(np.where(amax > 0, byte, 1), 1, 254)
    scaled = (w * np.exp2(127.0 - byte)[:, None, :]).reshape(k, n).astype(np.float32)
    by_word = np.ascontiguousarray(scaled.reshape(k // 512, 128, 4, n).transpose(0, 1, 3, 2))
    if fmt == "e4m3":
        words = by_word.astype(ml_dtypes.float8_e4m3fn).view(np.uint8)
    else:
        c = by_word.astype(ml_dtypes.float4_e2m1fn).view(np.uint8) & 0xF
        words = (c[..., 0::2] | (c[..., 1::2] << 4)).reshape(k // 512, 128, 2 * n)
    return np.ascontiguousarray(words), np.ascontiguousarray(byte.astype(np.uint8).reshape(k // 512, 16, n))


def unpack_weight(words, scales, fmt):
    g, _, n = scales.shape
    words = np.ascontiguousarray(words).reshape(g, 128, n, -1)
    if fmt == "e4m3":
        vals = words.view(ml_dtypes.float8_e4m3fn).astype(np.float64)
    else:
        nib = np.empty((g, 128, n, 4), np.uint8)
        nib[..., 0::2] = words & 0xF
        nib[..., 1::2] = words >> 4
        vals = E2M1[nib]
    vals = vals * np.repeat(np.exp2(scales.astype(np.float64) - 127.0), 8, axis=1)[..., None]
    return vals.transpose(0, 1, 3, 2).reshape(g * 512, n)


def gelu(v):
    return 0.5 * v * (1.0 + np.tanh(np.sqrt(2.0 / np.pi) * (v + 0.044715 * v**3)))


K, T, S, T2, H, N, P = 1024, 4096, 1024, 2048, 512, 768, 128


def setup_inputs():
    n = np.random.standard_normal
    s = mx_kscale(K)[:, None]
    u = mx_kscale(H)[:, None]
    tab_words, tab_scales = pack_weight(n((K, T)) * s, "e4m3")
    gain_words, gain_scales = pack_weight(n((H, N)) / np.sqrt(H) / u, "e2m1")
    return {
        "tab_words": tab_words,
        "tab_scales": tab_scales,
        "offs": striped(np.random.permutation(T)[:S]),
        "w1": (n((K, H)) / np.sqrt(K) / s * u.T).astype(np.float32),
        "b1": (0.5 * n(H) * u[:, 0]).astype(np.float32),
        "wgs": np.exp(0.3 * n((P, S))).astype(np.float32),
        "offs2": striped(np.random.permutation(T2)[:S]),
        "base": (n((H, T2)) * u).astype(np.float32),
        "gain_words": gain_words,
        "gain_scales": gain_scales,
        "lim": np.exp(0.3 * n(N)).astype(np.float32),
    }


def reference(tab_words, tab_scales, offs, w1, b1, wgs, offs2, base, gain_words, gain_scales, lim):
    v = unpack_weight(tab_words, tab_scales, "e4m3")[:, unstriped(offs)]
    w1q = mxq(f64(w1), 0, "e4m3")
    h = (w1q.T @ v) + f64(b1)[:, None]
    page = np.zeros((H, T2))
    page[:, unstriped(offs2)] = np.tile(f64(wgs), (H // P, 1)) * h
    z = page - f64(base)
    zq = mxq(z, 0, "e4m3")
    gain = unpack_weight(gain_words, gain_scales, "e2m1")
    d = gain.T @ zq
    return f64(lim)[:, None] * np.tanh(d)

@@ -1,0 +1,216 @@
+from contextlib import ExitStack
+
+import concourse.mybir as mybir
+
+K, T, S, T2, H, N, P = 1024, 4096, 1024, 2048, 512, 768, 128
+FLOPS = 2 * K * H * S + 2 * H * N * T2
+
+F32 = mybir.dt.float32
+BF16 = mybir.dt.bfloat16
+I32 = mybir.dt.int32
+U32 = mybir.dt.uint32
+U16 = mybir.dt.uint16
+U8 = mybir.dt.uint8
+FP8X4 = mybir.dt.float8_e4m3fn_x4
+FP4X4 = mybir.dt.float4_e2m1fn_x4
+ALU = mybir.AluOpType
+ACT = mybir.ActivationFunctionType
+
+PACK = 4
+PASSES = K // (P * PACK)
+HALF = S // 2
+GROUPS = N // P
+CHUNKS = (256, 256, 512, 512, 512)
+
+
+def tile_list_station_grid_increments_kernel(
+    tc, tab_words, tab_scales, offs, w1, b1, wgs, offs2, base, gain_words, gain_scales, lim, out
+):
+    nc = tc.nc
+    with ExitStack() as ctx:
+        keep = ctx.enter_context(tc.tile_pool(name="keep", bufs=1))
+        stage = ctx.enter_context(tc.tile_pool(name="stage", bufs=4))
+        res = ctx.enter_context(tc.tile_pool(name="res", bufs=12))
+        psum = ctx.enter_context(tc.psum_pool(name="psum", bufs=8))
+
+        pick = keep.tile([P, S // 16], U16, name="pick")
+        place = keep.tile([P, S // 16], U16, name="place")
+        table = [keep.tile([P, T], I32, name="table%d" % a, align_bytes=64) for a in range(PASSES)]
+        table_sc = keep.tile([P, T // 4], I32, name="table_sc", align_bytes=64)
+        picked = [keep.tile([P, S], U32, name="picked%d" % a, align_bytes=64) for a in range(PASSES)]
+        picked_sc = keep.tile([P, S], U8, name="picked_sc", align_bytes=64)
+        w_bf = [keep.tile([P, PACK * H], BF16, name="w_bf%d" % a, align_bytes=64) for a in range(PASSES)]
+        w_codes = [keep.tile([P, H], U32, name="w_codes%d" % a, align_bytes=64) for a in range(PASSES)]
+        w_sc = [keep.tile([P, H], U8, name="w_sc%d" % a, align_bytes=64) for a in range(PASSES)]
+        bias = keep.tile([P, PACK], F32, name="bias")
+        limit = keep.tile([P, GROUPS], F32, name="limit")
+        trust = [keep.tile([P, S], F32, name="trust%d" % t) for t in range(PACK)]
+        anomaly = [keep.tile([P, S], F32, name="anomaly%d" % t) for t in range(PACK)]
+        page = [keep.tile([P, T2], F32, name="page%d" % t) for t in range(PACK)]
+        z_rows = keep.tile([P, PACK, T2], BF16, name="z_rows", align_bytes=64)
+        z_packed = keep.tile([P, T2, PACK], BF16, name="z_packed", align_bytes=64)
+        z_codes = keep.tile([P, T2], U32, name="z_codes", align_bytes=64)
+        z_sc = keep.tile([P, T2], U8, name="z_sc", align_bytes=64)
+        gain = keep.tile([P, 2 * N], U8, name="gain", align_bytes=64)
+        gain_sc = keep.tile([P, N // 4], I32, name="gain_sc", align_bytes=64)
+
+        nc.vector.memset(table_sc[:], 0)
+        nc.vector.memset(gain_sc[:], 0)
+        for t in range(PACK):
+            nc.vector.memset(page[t][:], 0.0)
+
+        def load_w1(a):
+            raw = stage.tile([P, PACK * H], F32, name="stage")
+            rows = w1[a * P * PACK : (a + 1) * P * PACK, :]
+            nc.sync.dma_start(raw[:], rows.rearrange("(p j) c -> p (j c)", j=PACK))
+            return raw
+
+        def load_table(a):
+            nc.sync.dma_start(table[a][:], tab_words[a].rearrange("p n i -> p (n i)").bitcast(I32))
+
+        def load_table_scales(rows):
+            for r in rows:
+                for a in range(PASSES):
+                    src = tab_scales[a].rearrange("(q r) n -> r q n", r=4)[r]
+                    nc.sync.dma_start(table_sc[4 * a + r : P : 32, :], src.bitcast(I32))
+
+        def load_trust(t):
+            src = wgs.rearrange("(s t) j -> t s j", t=PACK)[t]
+            for q in (0, 2, 1, 3):
+                nc.sync.dma_start(trust[t][32 * q : 32 * (q + 1), :], src)
+
+        def load_base(t):
+            rows = stage.tile([P, T2], F32, name="stage")
+            nc.sync.dma_start(rows[:], base.rearrange("(p t) c -> t p c", t=PACK)[t])
+            return rows
+
+        w_raw = [load_w1(0)]
+        nc.sync.dma_start(pick[:], offs)
+        load_table_scales((0, 1))
+        w_raw.append(load_w1(1))
+        load_table(0)
+        load_table_scales((2, 3))
+        load_table(1)
+        nc.sync.dma_start(bias[:], b1.rearrange("(p t) -> p t", t=PACK))
+        nc.sync.dma_start(place[:], offs2)
+        load_trust(0)
+        load_trust(1)
+        base_rows = [load_base(0)]
+        load_trust(2)
+        base_rows.append(load_base(1))
+        load_trust(3)
+
+        for a in range(PASSES):
+            nc.scalar.copy(
+                w_bf[a][:].rearrange("p (t m j) -> p m t j", t=PACK, j=PACK),
+                w_raw[a][:].rearrange("p (j m t) -> p m t j", j=PACK, t=PACK),
+            )
+            nc.vector.quantize_mx(out=w_codes[a][:].bitcast(FP8X4), scales=w_sc[a][:], in_=w_bf[a][:])
+
+        base_rows.append(load_base(2))
+        base_rows.append(load_base(3))
+        nc.sync.dma_start(gain[:].bitcast(I32), gain_words[0].bitcast(I32))
+        for r in range(4):
+            src = gain_scales[0].rearrange("(q r) n -> r q n", r=4)[r]
+            nc.sync.dma_start(gain_sc[r:P:32, :], src.bitcast(I32))
+        with nc.allow_non_contiguous_dma(reason="one value for each partition and output group"):
+            nc.sync.dma_start(limit[:], lim.rearrange("(g p) -> p g", p=P))
+
+        halves = [slice(u * HALF, (u + 1) * HALF) for u in range(2)]
+        list_halves = [slice(u * HALF // 16, (u + 1) * HALF // 16) for u in range(2)]
+
+        nc.vector.tensor_copy(picked[0][:], table[0][:].bitcast(U32).indirect(pick[:]))
+        nc.vector.tensor_copy(picked_sc[:], table_sc[:].bitcast(U8).indirect(pick[:]))
+
+        def first_product(acc, a, t, u):
+            rows = slice(t * P, (t + 1) * P)
+            nc.tensor.matmul_mx(
+                out=acc[:],
+                lhsT=w_codes[a][:, rows].bitcast(FP8X4),
+                lhsT_scale=w_sc[a][:, rows],
+                rhs=picked[a][:, halves[u]].bitcast(FP8X4),
+                rhs_scale=picked_sc[4 * a : P, halves[u]],
+                start=(a == 0),
+                stop=(a == PASSES - 1),
+            )
+
+        h_acc = {}
+        for t in range(PACK):
+            for u in range(2):
+                h_acc[t, u] = psum.tile([P, HALF], F32, name="acc")
+                first_product(h_acc[t, u], 0, t, u)
+
+        for u in range(2):
+            nc.vector.tensor_copy(
+                picked[1][:, halves[u]], table[1][:].bitcast(U32).indirect(pick[:, list_halves[u]])
+            )
+        for t in range(PACK):
+            for u in range(2):
+                first_product(h_acc[t, u], 1, t, u)
+
+        def weigh(t, u):
+            dst = anomaly[t][:, halves[u]]
+            if (t, u) == (0, 0):
+                nc.vector.scalar_tensor_tensor(
+                    dst, h_acc[t, u][:], bias[:, t : t + 1], trust[t][:, halves[u]], ALU.add, ALU.mult
+                )
+            else:
+                nc.scalar.activation(dst, h_acc[t, u][:], ACT.Identity, bias=bias[:, t : t + 1])
+                nc.gpsimd.tensor_tensor(dst, dst, trust[t][:, halves[u]], ALU.mult)
+
+        def subtract(engine, t, cols):
+            engine.tensor_tensor(z_rows[:, t, cols], page[t][:, cols], base_rows[t][:, cols], ALU.subtract)
+
+        def pair_up(copy, first, cols):
+            copy(
+                z_packed[:, cols, first : first + 2],
+                z_rows[:, first : first + 2, cols].rearrange("p t c -> p c t"),
+            )
+
+        everything = slice(0, T2)
+        for u in range(2):
+            weigh(0, u)
+            nc.vector.tensor_copy(page[0][:].indirect(place[:, list_halves[u]]), anomaly[0][:, halves[u]])
+        for t in range(1, PACK):
+            for u in range(2):
+                weigh(t, u)
+            nc.vector.tensor_copy(page[t][:].indirect(place[:]), anomaly[t][:])
+            subtract(nc.gpsimd, t - 1, everything)
+
+        starts = [sum(CHUNKS[:i]) for i in range(len(CHUNKS))]
+        spans = [slice(s, s + w) for s, w in zip(starts, CHUNKS)]
+        for cols in spans:
+            pair_up(nc.scalar.copy, 0, cols)
+
+        def quantise_z(cols):
+            subtract(nc.vector, PACK - 1, cols)
+            pair_up(nc.vector.tensor_copy, 2, cols)
+            nc.vector.quantize_mx(
+                out=z_codes[:, cols].bitcast(FP8X4),
+                scales=z_sc[:, cols],
+                in_=z_packed[:, cols, :].rearrange("p c t -> p (c t)"),
+            )
+
+        def increments(cols):
+            width = cols.stop - cols.start
+            for g in range(GROUPS):
+                acc = psum.tile([P, width], F32, name="acc")
+                nc.tensor.matmul_mx(
+                    out=acc[:],
+                    lhsT=gain[:, 2 * P * g : 2 * P * (g + 1)].bitcast(FP4X4),
+                    lhsT_scale=gain_sc[:].bitcast(U8)[:, P * g : P * (g + 1)],
+                    rhs=z_codes[:, cols].bitcast(FP8X4),
+                    rhs_scale=z_sc[:, cols],
+                    start=True,
+                    stop=True,
+                )
+                result = res.tile([P, width], F32, name="result")
+                nc.scalar.activation(result[:], acc[:], ACT.Tanh)
+                nc.vector.tensor_scalar(result[:], result[:], limit[:, g : g + 1], None, ALU.mult)
+                nc.sync.dma_start(out[P * g : P * (g + 1), cols], result[:])
+
+        quantise_z(spans[0])
+        for i in range(len(spans)):
+            if i + 1 < len(spans):
+                quantise_z(spans[i + 1])
+            increments(spans[i])

@@ -21,6 +21,12 @@ PASSES = K // (P * PACK)
 HALF = S // 2
 GROUPS = N // P
 CHUNKS = (256, 256, 512, 512, 512)
+ROW = 4 * T2
+AT_TABLE = 0
+AT_RAW = AT_TABLE + 4 * T
+AT_PICKED = AT_RAW + 2 * ROW
+AT_SCALES = AT_PICKED + 4 * S
+AT_GAIN = AT_SCALES + T
 
 
 def tile_list_station_grid_increments_kernel(
@@ -29,98 +35,87 @@ def tile_list_station_grid_increments_kernel(
     nc = tc.nc
     with ExitStack() as ctx:
         keep = ctx.enter_context(tc.tile_pool(name="keep", bufs=1))
-        stage = ctx.enter_context(tc.tile_pool(name="stage", bufs=4))
-        res = ctx.enter_context(tc.tile_pool(name="res", bufs=12))
+        turns = ctx.enter_context(tc.tile_pool(name="turns", bufs=1))
+        res = ctx.enter_context(tc.tile_pool(name="res", bufs=30))
         psum = ctx.enter_context(tc.psum_pool(name="psum", bufs=8))
+
+        def tenant(shape, dtype, name, offset):
+            return turns.tile(shape, dtype, name=name, align_bytes=64, offset=offset)
 
         pick = keep.tile([P, S // 16], U16, name="pick")
         place = keep.tile([P, S // 16], U16, name="place")
-        table = [keep.tile([P, T], I32, name="table%d" % a, align_bytes=64) for a in range(PASSES)]
-        table_sc = keep.tile([P, T // 4], I32, name="table_sc", align_bytes=64)
-        picked = [keep.tile([P, S], U32, name="picked%d" % a, align_bytes=64) for a in range(PASSES)]
-        picked_sc = keep.tile([P, S], U8, name="picked_sc", align_bytes=64)
-        w_bf = [keep.tile([P, PACK * H], BF16, name="w_bf%d" % a, align_bytes=64) for a in range(PASSES)]
-        w_codes = [keep.tile([P, H], U32, name="w_codes%d" % a, align_bytes=64) for a in range(PASSES)]
-        w_sc = [keep.tile([P, H], U8, name="w_sc%d" % a, align_bytes=64) for a in range(PASSES)]
         bias = keep.tile([P, PACK], F32, name="bias")
-        limit = keep.tile([P, GROUPS], F32, name="limit")
-        trust = [keep.tile([P, S], F32, name="trust%d" % t) for t in range(PACK)]
+        picked_sc = keep.tile([P, S], U8, name="picked_sc", align_bytes=64)
         anomaly = [keep.tile([P, S], F32, name="anomaly%d" % t) for t in range(PACK)]
-        page = [keep.tile([P, T2], F32, name="page%d" % t) for t in range(PACK)]
         z_rows = keep.tile([P, PACK, T2], BF16, name="z_rows", align_bytes=64)
         z_packed = keep.tile([P, T2, PACK], BF16, name="z_packed", align_bytes=64)
         z_codes = keep.tile([P, T2], U32, name="z_codes", align_bytes=64)
         z_sc = keep.tile([P, T2], U8, name="z_sc", align_bytes=64)
-        gain = keep.tile([P, 2 * N], U8, name="gain", align_bytes=64)
-        gain_sc = keep.tile([P, N // 4], I32, name="gain_sc", align_bytes=64)
 
-        nc.vector.memset(table_sc[:], 0)
-        nc.vector.memset(gain_sc[:], 0)
-        for t in range(PACK):
-            nc.vector.memset(page[t][:], 0.0)
+        table = [tenant([P, T], I32, "table%d" % a, AT_TABLE) for a in range(PASSES)]
+        base_rows = [tenant([P, T2], F32, "base%d" % t, AT_TABLE + ROW * (t % 2)) for t in range(PACK)]
+        w_raw = [tenant([P, PACK * H], F32, "w_raw%d" % a, AT_RAW + ROW * a) for a in range(PASSES)]
+        page = [keep.tile([P, T2], F32, name="page%d" % t) for t in range(PACK)]
+        trust = [tenant([P, S], F32, "trust%d" % t, AT_RAW + 4 * S * t) for t in range(PACK - 1)]
+        trust.append(tenant([P, S], F32, "trust3", AT_PICKED))
+        w_bf = [keep.tile([P, PACK * H], BF16, name="w_bf%d" % a, align_bytes=64) for a in range(PASSES)]
+        table_sc = tenant([P, T // 4], I32, "table_sc", AT_SCALES)
+        picked = [keep.tile([P, S], U32, name="picked0", align_bytes=64), tenant([P, S], U32, "picked1", AT_PICKED)]
+        w_codes = [keep.tile([P, H], U32, name="w_codes0", align_bytes=64), tenant([P, H], U32, "w_codes1", AT_GAIN)]
+        w_sc = [keep.tile([P, H], U8, name="w_sc0", align_bytes=64), tenant([P, H], U8, "w_sc1", AT_SCALES)]
+        gain = tenant([P, 2 * N], U8, "gain", AT_GAIN)
+        limit = tenant([P, GROUPS], F32, "limit", AT_GAIN + 2 * N)
+        gain_sc = tenant([P, N // 4], I32, "gain_sc", AT_SCALES)
 
-        def load_w1(a):
-            raw = stage.tile([P, PACK * H], F32, name="stage")
-            rows = w1[a * P * PACK : (a + 1) * P * PACK, :]
-            nc.sync.dma_start(raw[:], rows.rearrange("(p j) c -> p (j c)", j=PACK))
-            return raw
+        halves = [slice(u * HALF, (u + 1) * HALF) for u in range(2)]
+        list_halves = [slice(u * HALF // 16, (u + 1) * HALF // 16) for u in range(2)]
 
         def load_table(a):
             nc.sync.dma_start(table[a][:], tab_words[a].rearrange("p n i -> p (n i)").bitcast(I32))
 
-        def load_table_scales(rows):
-            for r in rows:
-                for a in range(PASSES):
-                    src = tab_scales[a].rearrange("(q r) n -> r q n", r=4)[r]
-                    nc.sync.dma_start(table_sc[4 * a + r : P : 32, :], src.bitcast(I32))
-
-        def load_trust(t):
+        def load_trust(t, cols):
             src = wgs.rearrange("(s t) j -> t s j", t=PACK)[t]
             for q in (0, 2, 1, 3):
-                nc.sync.dma_start(trust[t][32 * q : 32 * (q + 1), :], src)
+                nc.sync.dma_start(trust[t][32 * q : 32 * (q + 1), cols], src[:, cols])
 
         def load_base(t):
-            rows = stage.tile([P, T2], F32, name="stage")
-            nc.sync.dma_start(rows[:], base.rearrange("(p t) c -> t p c", t=PACK)[t])
-            return rows
+            nc.sync.dma_start(base_rows[t][:], base.rearrange("(p t) c -> t p c", t=PACK)[t])
 
-        w_raw = [load_w1(0)]
-        nc.sync.dma_start(pick[:], offs)
-        load_table_scales((0, 1))
-        w_raw.append(load_w1(1))
-        load_table(0)
-        load_table_scales((2, 3))
-        load_table(1)
-        nc.sync.dma_start(bias[:], b1.rearrange("(p t) -> p t", t=PACK))
-        nc.sync.dma_start(place[:], offs2)
-        load_trust(0)
-        load_trust(1)
-        base_rows = [load_base(0)]
-        load_trust(2)
-        base_rows.append(load_base(1))
-        load_trust(3)
-
-        for a in range(PASSES):
+        def round_w1(a):
             nc.scalar.copy(
                 w_bf[a][:].rearrange("p (t m j) -> p m t j", t=PACK, j=PACK),
                 w_raw[a][:].rearrange("p (j m t) -> p m t j", j=PACK, t=PACK),
             )
             nc.vector.quantize_mx(out=w_codes[a][:].bitcast(FP8X4), scales=w_sc[a][:], in_=w_bf[a][:])
 
-        base_rows.append(load_base(2))
-        base_rows.append(load_base(3))
-        nc.sync.dma_start(gain[:].bitcast(I32), gain_words[0].bitcast(I32))
-        for r in range(4):
-            src = gain_scales[0].rearrange("(q r) n -> r q n", r=4)[r]
-            nc.sync.dma_start(gain_sc[r:P:32, :], src.bitcast(I32))
-        with nc.allow_non_contiguous_dma(reason="one value for each partition and output group"):
-            nc.sync.dma_start(limit[:], lim.rearrange("(g p) -> p g", p=P))
-
-        halves = [slice(u * HALF, (u + 1) * HALF) for u in range(2)]
-        list_halves = [slice(u * HALF // 16, (u + 1) * HALF // 16) for u in range(2)]
+        nc.gpsimd.memset(table_sc[:], 0)
+        nc.gpsimd.memset(page[PACK - 1][:], 0.0)
+        nc.sync.dma_start(pick[:], offs)
+        nc.sync.dma_start(place[:], offs2)
+        nc.sync.dma_start(bias[:], b1.rearrange("(p t) -> p t", t=PACK))
+        load_table(0)
+        for a in range(PASSES):
+            rows = w1[a * P * PACK : (a + 1) * P * PACK, :]
+            nc.sync.dma_start(w_raw[a][:], rows.rearrange("(p j) c -> p (j c)", j=PACK))
+        for q in (0, 2):
+            src = tab_scales[:, 4 * q : 4 * (q + 1), :]
+            nc.sync.dma_start(table_sc[32 * q : 32 * q + 4 * PASSES, :], src.bitcast(I32))
+        for q in (1, 3):
+            for a in range(PASSES):
+                src = tab_scales[a, 4 * q : 4 * (q + 1), :]
+                nc.sync.dma_start(table_sc[32 * q + 4 * a : 32 * q + 4 * (a + 1), :], src.bitcast(I32))
 
         nc.vector.tensor_copy(picked[0][:], table[0][:].bitcast(U32).indirect(pick[:]))
+        load_table(1)
         nc.vector.tensor_copy(picked_sc[:], table_sc[:].bitcast(U8).indirect(pick[:]))
+        for a in range(PASSES):
+            round_w1(a)
+        for t in range(PACK - 1):
+            nc.vector.memset(page[t][:], 0.0)
+        load_trust(0, halves[0])
+        load_trust(0, halves[1])
+        load_trust(1, slice(0, S))
+        load_trust(2, slice(0, S))
 
         def first_product(acc, a, t, u):
             rows = slice(t * P, (t + 1) * P)
@@ -148,15 +143,22 @@ def tile_list_station_grid_increments_kernel(
             for u in range(2):
                 first_product(h_acc[t, u], 1, t, u)
 
-        def weigh(t, u):
-            dst = anomaly[t][:, halves[u]]
-            if (t, u) == (0, 0):
-                nc.vector.scalar_tensor_tensor(
-                    dst, h_acc[t, u][:], bias[:, t : t + 1], trust[t][:, halves[u]], ALU.add, ALU.mult
-                )
-            else:
-                nc.scalar.activation(dst, h_acc[t, u][:], ACT.Identity, bias=bias[:, t : t + 1])
-                nc.gpsimd.tensor_tensor(dst, dst, trust[t][:, halves[u]], ALU.mult)
+        load_base(0)
+        load_base(1)
+        load_trust(3, slice(0, S))
+        nc.gpsimd.memset(gain_sc[:], 0)
+        nc.sync.dma_start(gain[:].bitcast(I32), gain_words[0].bitcast(I32))
+        for r in range(4):
+            src = gain_scales[0].rearrange("(q r) n -> r q n", r=4)[r]
+            nc.sync.dma_start(gain_sc[r:P:32, :], src.bitcast(I32))
+        with nc.allow_non_contiguous_dma(reason="one value for each partition and output group"):
+            nc.sync.dma_start(limit[:], lim.rearrange("(g p) -> p g", p=P))
+
+        def add_bias(t, u):
+            nc.scalar.activation(anomaly[t][:, halves[u]], h_acc[t, u][:], ACT.Identity, bias=bias[:, t : t + 1])
+
+        def weigh(t, cols):
+            nc.gpsimd.tensor_tensor(anomaly[t][:, cols], anomaly[t][:, cols], trust[t][:, cols], ALU.mult)
 
         def subtract(engine, t, cols):
             engine.tensor_tensor(z_rows[:, t, cols], page[t][:, cols], base_rows[t][:, cols], ALU.subtract)
@@ -167,15 +169,24 @@ def tile_list_station_grid_increments_kernel(
                 z_rows[:, first : first + 2, cols].rearrange("p t c -> p c t"),
             )
 
-        everything = slice(0, T2)
-        for u in range(2):
-            weigh(0, u)
-            nc.vector.tensor_copy(page[0][:].indirect(place[:, list_halves[u]]), anomaly[0][:, halves[u]])
+        nc.vector.scalar_tensor_tensor(
+            anomaly[0][:, halves[0]], h_acc[0, 0][:], bias[:, 0:1], trust[0][:, halves[0]], ALU.add, ALU.mult
+        )
+        add_bias(0, 1)
+        weigh(0, halves[1])
         for t in range(1, PACK):
             for u in range(2):
-                weigh(t, u)
+                add_bias(t, u)
+            weigh(t, slice(0, S))
+        for u in range(2):
+            nc.vector.tensor_copy(page[0][:].indirect(place[:, list_halves[u]]), anomaly[0][:, halves[u]])
+        for t in range(1, PACK):
             nc.vector.tensor_copy(page[t][:].indirect(place[:]), anomaly[t][:])
-            subtract(nc.gpsimd, t - 1, everything)
+        for t in range(PACK - 1):
+            for v in range(2):
+                subtract(nc.gpsimd, t, slice(v * T2 // 2, (v + 1) * T2 // 2))
+            if t + 2 < PACK:
+                load_base(t + 2)
 
         starts = [sum(CHUNKS[:i]) for i in range(len(CHUNKS))]
         spans = [slice(s, s + w) for s, w in zip(starts, CHUNKS)]

@@ -26,7 +26,7 @@ AT_TABLE = 0
 AT_RAW = AT_TABLE + 4 * T
 AT_PICKED = AT_RAW + 2 * ROW
 AT_SCALES = AT_PICKED + 4 * S
-AT_GAIN = AT_SCALES + T
+AT_GAIN = AT_SCALES + 2 * H
 
 
 def tile_list_station_grid_increments_kernel(
@@ -45,7 +45,7 @@ def tile_list_station_grid_increments_kernel(
         pick = keep.tile([P, S // 16], U16, name="pick")
         place = keep.tile([P, S // 16], U16, name="place")
         bias = keep.tile([P, PACK], F32, name="bias")
-        picked_sc = keep.tile([P, S], U8, name="picked_sc", align_bytes=64)
+        picked_sc = keep.tile([P, S // 4], I32, name="picked_sc", align_bytes=64)
         anomaly = [keep.tile([P, S], F32, name="anomaly%d" % t) for t in range(PACK)]
         z_rows = keep.tile([P, PACK, T2], BF16, name="z_rows", align_bytes=64)
         z_packed = keep.tile([P, T2, PACK], BF16, name="z_packed", align_bytes=64)
@@ -59,7 +59,8 @@ def tile_list_station_grid_increments_kernel(
         trust = [tenant([P, S], F32, "trust%d" % t, AT_RAW + 4 * S * t) for t in range(PACK - 1)]
         trust.append(tenant([P, S], F32, "trust3", AT_PICKED))
         w_bf = [keep.tile([P, PACK * H], BF16, name="w_bf%d" % a, align_bytes=64) for a in range(PASSES)]
-        table_sc = tenant([P, T // 4], I32, "table_sc", AT_SCALES)
+        table_sc = tenant([P, T // 4], I32, "table_sc", AT_RAW + ROW)
+        picked_rows = keep.tile([P, S], U8, name="picked_rows", align_bytes=64)
         picked = [keep.tile([P, S], U32, name="picked0", align_bytes=64), tenant([P, S], U32, "picked1", AT_PICKED)]
         w_codes = [keep.tile([P, H], U32, name="w_codes0", align_bytes=64), tenant([P, H], U32, "w_codes1", AT_GAIN)]
         w_sc = [keep.tile([P, H], U8, name="w_sc0", align_bytes=64), tenant([P, H], U8, "w_sc1", AT_SCALES)]
@@ -88,30 +89,35 @@ def tile_list_station_grid_increments_kernel(
             )
             nc.vector.quantize_mx(out=w_codes[a][:].bitcast(FP8X4), scales=w_sc[a][:], in_=w_bf[a][:])
 
-        nc.gpsimd.memset(table_sc[:], 0)
-        nc.gpsimd.memset(page[PACK - 1][:], 0.0)
-        nc.sync.dma_start(pick[:], offs)
-        nc.sync.dma_start(place[:], offs2)
-        nc.sync.dma_start(bias[:], b1.rearrange("(p t) -> p t", t=PACK))
-        load_table(0)
-        for a in range(PASSES):
+        def load_w1(a):
             rows = w1[a * P * PACK : (a + 1) * P * PACK, :]
             nc.sync.dma_start(w_raw[a][:], rows.rearrange("(p j) c -> p (j c)", j=PACK))
-        for q in (0, 2):
-            src = tab_scales[:, 4 * q : 4 * (q + 1), :]
-            nc.sync.dma_start(table_sc[32 * q : 32 * q + 4 * PASSES, :], src.bitcast(I32))
-        for q in (1, 3):
-            for a in range(PASSES):
-                src = tab_scales[a, 4 * q : 4 * (q + 1), :]
-                nc.sync.dma_start(table_sc[32 * q + 4 * a : 32 * q + 4 * (a + 1), :], src.bitcast(I32))
 
+        def place_scales(a):
+            for q in range(4):
+                src = picked_rows[:].bitcast(I32)[16 * a + 4 * q : 16 * a + 4 * (q + 1), :]
+                nc.sync.dma_start(picked_sc[32 * q + 4 * a : 32 * q + 4 * (a + 1), :], src)
+
+        nc.sync.dma_start(table_sc[0:32, :], tab_scales.rearrange("a q n -> (a q) n").bitcast(I32))
+        nc.sync.dma_start(pick[:], offs)
+        load_table(0)
+        nc.sync.dma_start(place[:], offs2)
+        nc.sync.dma_start(bias[:], b1.rearrange("(p t) -> p t", t=PACK))
+        load_w1(0)
+        nc.gpsimd.memset(table_sc[64:P, :], 0)
+        nc.vector.memset(table_sc[32:64, :], 0)
+        nc.vector.memset(picked_sc[:], 0)
+
+        nc.vector.tensor_copy(picked_rows[:], table_sc[:].bitcast(U8).indirect(pick[:]))
+        place_scales(0)
+        load_w1(1)
+        place_scales(1)
         nc.vector.tensor_copy(picked[0][:], table[0][:].bitcast(U32).indirect(pick[:]))
         load_table(1)
-        nc.vector.tensor_copy(picked_sc[:], table_sc[:].bitcast(U8).indirect(pick[:]))
         for a in range(PASSES):
             round_w1(a)
-        for t in range(PACK - 1):
-            nc.vector.memset(page[t][:], 0.0)
+        for t in range(PACK):
+            nc.gpsimd.memset(page[t][:], 0.0)
         load_trust(0, halves[0])
         load_trust(0, halves[1])
         load_trust(1, slice(0, S))
@@ -124,7 +130,7 @@ def tile_list_station_grid_increments_kernel(
                 lhsT=w_codes[a][:, rows].bitcast(FP8X4),
                 lhsT_scale=w_sc[a][:, rows],
                 rhs=picked[a][:, halves[u]].bitcast(FP8X4),
-                rhs_scale=picked_sc[4 * a : P, halves[u]],
+                rhs_scale=picked_sc[:].bitcast(U8)[4 * a : P, halves[u]],
                 start=(a == 0),
                 stop=(a == PASSES - 1),
             )

@@ -104,7 +104,7 @@ def tile_list_station_grid_increments_kernel(
         nc.sync.dma_start(place[:], offs2)
         nc.sync.dma_start(bias[:], b1.rearrange("(p t) -> p t", t=PACK))
         load_w1(0)
-        nc.gpsimd.memset(table_sc[64:P, :], 0)
+        nc.vector.memset(table_sc[64:P, :], 0)
         nc.vector.memset(table_sc[32:64, :], 0)
         nc.vector.memset(picked_sc[:], 0)
 
@@ -117,7 +117,7 @@ def tile_list_station_grid_increments_kernel(
         for a in range(PASSES):
             round_w1(a)
         for t in range(PACK):
-            nc.gpsimd.memset(page[t][:], 0.0)
+            nc.vector.memset(page[t][:], 0.0)
         load_trust(0, halves[0])
         load_trust(0, halves[1])
         load_trust(1, slice(0, S))

@@ -27,6 +27,8 @@ AT_RAW = AT_TABLE + 4 * T
 AT_PICKED = AT_RAW + 2 * ROW
 AT_SCALES = AT_PICKED + 4 * S
 AT_GAIN = AT_SCALES + 2 * H
+AT_ROUNDED = AT_GAIN + 4 * H
+AT_ROWS = AT_ROUNDED + 4 * S
 
 
 def tile_list_station_grid_increments_kernel(
@@ -36,7 +38,7 @@ def tile_list_station_grid_increments_kernel(
     with ExitStack() as ctx:
         keep = ctx.enter_context(tc.tile_pool(name="keep", bufs=1))
         turns = ctx.enter_context(tc.tile_pool(name="turns", bufs=1))
-        res = ctx.enter_context(tc.tile_pool(name="res", bufs=30))
+        res = ctx.enter_context(tc.tile_pool(name="res", bufs=31))
         psum = ctx.enter_context(tc.psum_pool(name="psum", bufs=8))
 
         def tenant(shape, dtype, name, offset):
@@ -44,7 +46,6 @@ def tile_list_station_grid_increments_kernel(
 
         pick = keep.tile([P, S // 16], U16, name="pick")
         place = keep.tile([P, S // 16], U16, name="place")
-        bias = keep.tile([P, PACK], F32, name="bias")
         picked_sc = keep.tile([P, S // 4], I32, name="picked_sc", align_bytes=64)
         anomaly = [keep.tile([P, S], F32, name="anomaly%d" % t) for t in range(PACK)]
         z_rows = keep.tile([P, PACK, T2], BF16, name="z_rows", align_bytes=64)
@@ -55,12 +56,17 @@ def tile_list_station_grid_increments_kernel(
         table = [tenant([P, T], I32, "table%d" % a, AT_TABLE) for a in range(PASSES)]
         base_rows = [tenant([P, T2], F32, "base%d" % t, AT_TABLE + ROW * (t % 2)) for t in range(PACK)]
         w_raw = [tenant([P, PACK * H], F32, "w_raw%d" % a, AT_RAW + ROW * a) for a in range(PASSES)]
-        page = [keep.tile([P, T2], F32, name="page%d" % t) for t in range(PACK)]
-        trust = [tenant([P, S], F32, "trust%d" % t, AT_RAW + 4 * S * t) for t in range(PACK - 1)]
-        trust.append(tenant([P, S], F32, "trust3", AT_PICKED))
-        w_bf = [keep.tile([P, PACK * H], BF16, name="w_bf%d" % a, align_bytes=64) for a in range(PASSES)]
+        page = [keep.tile([P, T2], F32, name="page%d" % t) for t in range(PACK - 1)]
+        page.append(tenant([P, T2], F32, "page3", AT_RAW))
+        trust_at = (AT_ROUNDED, AT_RAW + ROW, AT_RAW + ROW + 4 * S, AT_PICKED)
+        trust = [tenant([P, S], F32, "trust%d" % t, trust_at[t]) for t in range(PACK)]
+        w_bf = [
+            tenant([P, PACK * H], BF16, "w_bf0", AT_ROUNDED),
+            keep.tile([P, PACK * H], BF16, name="w_bf1", align_bytes=64),
+        ]
         table_sc = tenant([P, T // 4], I32, "table_sc", AT_RAW + ROW)
-        picked_rows = keep.tile([P, S], U8, name="picked_rows", align_bytes=64)
+        picked_rows = tenant([P, S], U8, "picked_rows", AT_ROWS)
+        bias = tenant([P, PACK], F32, "bias", AT_ROWS)
         picked = [keep.tile([P, S], U32, name="picked0", align_bytes=64), tenant([P, S], U32, "picked1", AT_PICKED)]
         w_codes = [keep.tile([P, H], U32, name="w_codes0", align_bytes=64), tenant([P, H], U32, "w_codes1", AT_GAIN)]
         w_sc = [keep.tile([P, H], U8, name="w_sc0", align_bytes=64), tenant([P, H], U8, "w_sc1", AT_SCALES)]
@@ -102,7 +108,6 @@ def tile_list_station_grid_increments_kernel(
         nc.sync.dma_start(pick[:], offs)
         load_table(0)
         nc.sync.dma_start(place[:], offs2)
-        nc.sync.dma_start(bias[:], b1.rearrange("(p t) -> p t", t=PACK))
         load_w1(0)
         nc.vector.memset(table_sc[64:P, :], 0)
         nc.vector.memset(table_sc[32:64, :], 0)
@@ -114,6 +119,7 @@ def tile_list_station_grid_increments_kernel(
         place_scales(1)
         nc.vector.tensor_copy(picked[0][:], table[0][:].bitcast(U32).indirect(pick[:]))
         load_table(1)
+        nc.sync.dma_start(bias[:], b1.rearrange("(p t) -> p t", t=PACK))
         for a in range(PASSES):
             round_w1(a)
         for t in range(PACK):
@@ -221,10 +227,13 @@ def tile_list_station_grid_increments_kernel(
                     start=True,
                     stop=True,
                 )
-                result = res.tile([P, width], F32, name="result")
-                nc.scalar.activation(result[:], acc[:], ACT.Tanh)
-                nc.vector.tensor_scalar(result[:], result[:], limit[:, g : g + 1], None, ALU.mult)
-                nc.sync.dma_start(out[P * g : P * (g + 1), cols], result[:])
+                pieces = 2 if (cols.stop, g) == (T2, GROUPS - 1) else 1
+                step = width // pieces
+                for lo in range(0, width, step):
+                    result = res.tile([P, step], F32, name="result")
+                    nc.scalar.activation(result[:], acc[:, lo : lo + step], ACT.Tanh)
+                    nc.vector.tensor_scalar(result[:], result[:], limit[:, g : g + 1], None, ALU.mult)
+                    nc.sync.dma_start(out[P * g : P * (g + 1), cols.start + lo : cols.start + lo + step], result[:])
 
         quantise_z(spans[0])
         for i in range(len(spans)):

@@ -22,8 +22,10 @@ HALF = S // 2
 GROUPS = N // P
 CHUNKS = (256, 256, 512, 512, 512)
 ROW = 4 * T2
-AT_TABLE = 0
-AT_RAW = AT_TABLE + 4 * T
+LAP = 64
+AT_TABLE = (2 * LAP, 2 * ROW + LAP)
+AT_BASE = 2 * ROW
+AT_RAW = AT_BASE + 3 * ROW
 AT_PICKED = AT_RAW + 2 * ROW
 AT_SCALES = AT_PICKED + 4 * S
 AT_GAIN = AT_SCALES + 2 * H
@@ -53,11 +55,11 @@ def tile_list_station_grid_increments_kernel(
         z_codes = keep.tile([P, T2], U32, name="z_codes", align_bytes=64)
         z_sc = keep.tile([P, T2], U8, name="z_sc", align_bytes=64)
 
-        table = [tenant([P, T], I32, "table%d" % a, AT_TABLE) for a in range(PASSES)]
-        base_rows = [tenant([P, T2], F32, "base%d" % t, AT_TABLE + ROW * (t % 2)) for t in range(PACK)]
+        table = [tenant([P, T], I32, "table%d" % a, AT_TABLE[a]) for a in range(PASSES)]
+        base_rows = [tenant([P, T2], F32, "base%d" % t, AT_BASE + ROW * (t % 2)) for t in range(PACK)]
         w_raw = [tenant([P, PACK * H], F32, "w_raw%d" % a, AT_RAW + ROW * a) for a in range(PASSES)]
-        page = [keep.tile([P, T2], F32, name="page%d" % t) for t in range(PACK - 1)]
-        page.append(tenant([P, T2], F32, "page3", AT_RAW))
+        page_at = (0, ROW, AT_RAW, AT_BASE + 2 * ROW)
+        page = [tenant([P, T2], F32, "page%d" % t, page_at[t]) for t in range(PACK)]
         trust_at = (AT_ROUNDED, AT_RAW + ROW, AT_RAW + ROW + 4 * S, AT_PICKED)
         trust = [tenant([P, S], F32, "trust%d" % t, trust_at[t]) for t in range(PACK)]
         w_bf = [
@@ -122,7 +124,7 @@ def tile_list_station_grid_increments_kernel(
         nc.sync.dma_start(bias[:], b1.rearrange("(p t) -> p t", t=PACK))
         for a in range(PASSES):
             round_w1(a)
-        for t in range(PACK):
+        for t in range(PACK - 1):
             nc.vector.memset(page[t][:], 0.0)
         load_trust(0, halves[0])
         load_trust(0, halves[1])
@@ -155,6 +157,7 @@ def tile_list_station_grid_increments_kernel(
             for u in range(2):
                 first_product(h_acc[t, u], 1, t, u)
 
+        nc.gpsimd.memset(page[PACK - 1][:], 0.0)
         load_base(0)
         load_base(1)
         load_trust(3, slice(0, S))

@@ -22,15 +22,17 @@ HALF = S // 2
 GROUPS = N // P
 CHUNKS = (256, 256, 512, 512, 512)
 ROW = 4 * T2
-LAP = 64
-AT_TABLE = (2 * LAP, 2 * ROW + LAP)
-AT_BASE = 2 * ROW
-AT_RAW = AT_BASE + 3 * ROW
-AT_PICKED = AT_RAW + 2 * ROW
-AT_SCALES = AT_PICKED + 4 * S
+AT_TABLE0 = 0
+AT_BIAS = AT_TABLE0 + 2 * ROW
+AT_PAGE2 = AT_BIAS + 64
+AT_RAW0 = AT_PAGE2 + ROW // 2
+AT_PAGE3 = AT_PAGE2 + ROW
+AT_RAW1 = AT_PAGE3 + ROW
+AT_TABLE1 = AT_RAW1 + ROW
+AT_PICKED = AT_TABLE1 + 2 * ROW
+AT_SCALES = AT_PICKED + ROW
 AT_GAIN = AT_SCALES + 2 * H
 AT_ROUNDED = AT_GAIN + 4 * H
-AT_ROWS = AT_ROUNDED + 4 * S
 
 
 def tile_list_station_grid_increments_kernel(
@@ -48,27 +50,28 @@ def tile_list_station_grid_increments_kernel(
 
         pick = keep.tile([P, S // 16], U16, name="pick")
         place = keep.tile([P, S // 16], U16, name="place")
-        picked_sc = keep.tile([P, S // 4], I32, name="picked_sc", align_bytes=64)
+        picked_sc = [keep.tile([P, S // 4], I32, name="picked_sc%d" % a, align_bytes=64) for a in range(PASSES)]
         anomaly = [keep.tile([P, S], F32, name="anomaly%d" % t) for t in range(PACK)]
         z_rows = keep.tile([P, PACK, T2], BF16, name="z_rows", align_bytes=64)
         z_packed = keep.tile([P, T2, PACK], BF16, name="z_packed", align_bytes=64)
         z_codes = keep.tile([P, T2], U32, name="z_codes", align_bytes=64)
         z_sc = keep.tile([P, T2], U8, name="z_sc", align_bytes=64)
 
-        table = [tenant([P, T], I32, "table%d" % a, AT_TABLE[a]) for a in range(PASSES)]
-        base_rows = [tenant([P, T2], F32, "base%d" % t, AT_BASE + ROW * (t % 2)) for t in range(PACK)]
-        w_raw = [tenant([P, PACK * H], F32, "w_raw%d" % a, AT_RAW + ROW * a) for a in range(PASSES)]
-        page_at = (0, ROW, AT_RAW, AT_BASE + 2 * ROW)
-        page = [tenant([P, T2], F32, "page%d" % t, page_at[t]) for t in range(PACK)]
-        trust_at = (AT_ROUNDED, AT_RAW + ROW, AT_RAW + ROW + 4 * S, AT_PICKED)
+        table = [tenant([P, T], I32, "table0", AT_TABLE0 + 64), tenant([P, T], I32, "table1", AT_TABLE1)]
+        bias = tenant([P, PACK], F32, "bias", AT_BIAS)
+        base_rows = [tenant([P, T2], F32, "base%d" % t, (AT_TABLE1, AT_PICKED)[t % 2]) for t in range(PACK)]
+        w_raw = [tenant([P, PACK * H], F32, "w_raw%d" % a, (AT_RAW0, AT_RAW1)[a]) for a in range(PASSES)]
+        page_at = (AT_TABLE0 + ROW, AT_PAGE2, AT_PAGE3)
+        page = [keep.tile([P, T2], F32, name="page0")]
+        page.extend(tenant([P, T2], F32, "page%d" % t, page_at[t - 1]) for t in range(1, PACK))
+        trust_at = (AT_ROUNDED, AT_RAW1, AT_RAW1 + 4 * S, AT_TABLE1 + ROW)
         trust = [tenant([P, S], F32, "trust%d" % t, trust_at[t]) for t in range(PACK)]
         w_bf = [
             tenant([P, PACK * H], BF16, "w_bf0", AT_ROUNDED),
             keep.tile([P, PACK * H], BF16, name="w_bf1", align_bytes=64),
         ]
-        table_sc = tenant([P, T // 4], I32, "table_sc", AT_RAW + ROW)
-        picked_rows = tenant([P, S], U8, "picked_rows", AT_ROWS)
-        bias = tenant([P, PACK], F32, "bias", AT_ROWS)
+        table_sc = tenant([P, T // 4], I32, "table_sc", AT_TABLE1 - T // 2)
+        picked_rows = keep.tile([P, S], U8, name="picked_rows", align_bytes=64)
         picked = [keep.tile([P, S], U32, name="picked0", align_bytes=64), tenant([P, S], U32, "picked1", AT_PICKED)]
         w_codes = [keep.tile([P, H], U32, name="w_codes0", align_bytes=64), tenant([P, H], U32, "w_codes1", AT_GAIN)]
         w_sc = [keep.tile([P, H], U8, name="w_sc0", align_bytes=64), tenant([P, H], U8, "w_sc1", AT_SCALES)]
@@ -104,7 +107,7 @@ def tile_list_station_grid_increments_kernel(
         def place_scales(a):
             for q in range(4):
                 src = picked_rows[:].bitcast(I32)[16 * a + 4 * q : 16 * a + 4 * (q + 1), :]
-                nc.sync.dma_start(picked_sc[32 * q + 4 * a : 32 * q + 4 * (a + 1), :], src)
+                nc.sync.dma_start(picked_sc[a][32 * q : 32 * q + 4, :], src)
 
         nc.sync.dma_start(table_sc[0:32, :], tab_scales.rearrange("a q n -> (a q) n").bitcast(I32))
         nc.sync.dma_start(pick[:], offs)
@@ -113,18 +116,19 @@ def tile_list_station_grid_increments_kernel(
         load_w1(0)
         nc.vector.memset(table_sc[64:P, :], 0)
         nc.vector.memset(table_sc[32:64, :], 0)
-        nc.vector.memset(picked_sc[:], 0)
+        for a in range(PASSES):
+            nc.vector.memset(picked_sc[a][:], 0)
 
         nc.vector.tensor_copy(picked_rows[:], table_sc[:].bitcast(U8).indirect(pick[:]))
         place_scales(0)
         load_w1(1)
+        load_table(1)
         place_scales(1)
         nc.vector.tensor_copy(picked[0][:], table[0][:].bitcast(U32).indirect(pick[:]))
-        load_table(1)
         nc.sync.dma_start(bias[:], b1.rearrange("(p t) -> p t", t=PACK))
         for a in range(PASSES):
             round_w1(a)
-        for t in range(PACK - 1):
+        for t in range(PACK):
             nc.vector.memset(page[t][:], 0.0)
         load_trust(0, halves[0])
         load_trust(0, halves[1])
@@ -138,7 +142,7 @@ def tile_list_station_grid_increments_kernel(
                 lhsT=w_codes[a][:, rows].bitcast(FP8X4),
                 lhsT_scale=w_sc[a][:, rows],
                 rhs=picked[a][:, halves[u]].bitcast(FP8X4),
-                rhs_scale=picked_sc[:].bitcast(U8)[4 * a : P, halves[u]],
+                rhs_scale=picked_sc[a][:].bitcast(U8)[:, halves[u]],
                 start=(a == 0),
                 stop=(a == PASSES - 1),
             )
@@ -157,10 +161,9 @@ def tile_list_station_grid_increments_kernel(
             for u in range(2):
                 first_product(h_acc[t, u], 1, t, u)
 
-        nc.gpsimd.memset(page[PACK - 1][:], 0.0)
         load_base(0)
-        load_base(1)
         load_trust(3, slice(0, S))
+        load_base(1)
         nc.gpsimd.memset(gain_sc[:], 0)
         nc.sync.dma_start(gain[:].bitcast(I32), gain_words[0].bitcast(I32))
         for r in range(4):
@@ -198,8 +201,9 @@ def tile_list_station_grid_increments_kernel(
         for t in range(1, PACK):
             nc.vector.tensor_copy(page[t][:].indirect(place[:]), anomaly[t][:])
         for t in range(PACK - 1):
-            for v in range(2):
-                subtract(nc.gpsimd, t, slice(v * T2 // 2, (v + 1) * T2 // 2))
+            pieces = 1 if t == 0 else 2
+            for v in range(pieces):
+                subtract(nc.gpsimd, t, slice(v * T2 // pieces, (v + 1) * T2 // pieces))
             if t + 2 < PACK:
                 load_base(t + 2)
 

@@ -23,8 +23,7 @@ GROUPS = N // P
 CHUNKS = (256, 256, 512, 512, 512)
 ROW = 4 * T2
 AT_TABLE0 = 0
-AT_BIAS = AT_TABLE0 + 2 * ROW
-AT_PAGE2 = AT_BIAS + 64
+AT_PAGE2 = AT_TABLE0 + 2 * ROW
 AT_RAW0 = AT_PAGE2 + ROW // 2
 AT_PAGE3 = AT_PAGE2 + ROW
 AT_RAW1 = AT_PAGE3 + ROW
@@ -57,14 +56,14 @@ def tile_list_station_grid_increments_kernel(
         z_codes = keep.tile([P, T2], U32, name="z_codes", align_bytes=64)
         z_sc = keep.tile([P, T2], U8, name="z_sc", align_bytes=64)
 
-        table = [tenant([P, T], I32, "table0", AT_TABLE0 + 64), tenant([P, T], I32, "table1", AT_TABLE1)]
-        bias = tenant([P, PACK], F32, "bias", AT_BIAS)
+        table = [tenant([P, T], I32, "table0", AT_TABLE0), tenant([P, T], I32, "table1", AT_TABLE1)]
+        bias = tenant([P, PACK], F32, "bias", AT_ROUNDED)
         base_rows = [tenant([P, T2], F32, "base%d" % t, (AT_TABLE1, AT_PICKED)[t % 2]) for t in range(PACK)]
         w_raw = [tenant([P, PACK * H], F32, "w_raw%d" % a, (AT_RAW0, AT_RAW1)[a]) for a in range(PASSES)]
         page_at = (AT_TABLE0 + ROW, AT_PAGE2, AT_PAGE3)
         page = [keep.tile([P, T2], F32, name="page0")]
         page.extend(tenant([P, T2], F32, "page%d" % t, page_at[t - 1]) for t in range(1, PACK))
-        trust_at = (AT_ROUNDED, AT_RAW1, AT_RAW1 + 4 * S, AT_TABLE1 + ROW)
+        trust_at = (AT_ROUNDED + 64, AT_RAW1, AT_RAW1 + 4 * S, AT_TABLE1 + ROW)
         trust = [tenant([P, S], F32, "trust%d" % t, trust_at[t]) for t in range(PACK)]
         w_bf = [
             tenant([P, PACK * H], BF16, "w_bf0", AT_ROUNDED),
@@ -111,9 +110,9 @@ def tile_list_station_grid_increments_kernel(
 
         nc.sync.dma_start(table_sc[0:32, :], tab_scales.rearrange("a q n -> (a q) n").bitcast(I32))
         nc.sync.dma_start(pick[:], offs)
+        load_w1(0)
         load_table(0)
         nc.sync.dma_start(place[:], offs2)
-        load_w1(0)
         nc.vector.memset(table_sc[64:P, :], 0)
         nc.vector.memset(table_sc[32:64, :], 0)
         for a in range(PASSES):
@@ -125,11 +124,11 @@ def tile_list_station_grid_increments_kernel(
         load_table(1)
         place_scales(1)
         nc.vector.tensor_copy(picked[0][:], table[0][:].bitcast(U32).indirect(pick[:]))
-        nc.sync.dma_start(bias[:], b1.rearrange("(p t) -> p t", t=PACK))
         for a in range(PASSES):
             round_w1(a)
         for t in range(PACK):
             nc.vector.memset(page[t][:], 0.0)
+        nc.sync.dma_start(bias[:], b1.rearrange("(p t) -> p t", t=PACK))
         load_trust(0, halves[0])
         load_trust(0, halves[1])
         load_trust(1, slice(0, S))

@@ -213,7 +213,7 @@ def tile_list_station_grid_increments_kernel(
 
         def quantise_z(cols):
             subtract(nc.vector, PACK - 1, cols)
-            pair_up(nc.vector.tensor_copy, 2, cols)
+            pair_up(nc.scalar.copy if cols == spans[1] else nc.vector.tensor_copy, 2, cols)
             nc.vector.quantize_mx(
                 out=z_codes[:, cols].bitcast(FP8X4),
                 scales=z_sc[:, cols],

@@ -25,13 +25,13 @@ ROW = 4 * T2
 AT_TABLE0 = 0
 AT_PAGE2 = AT_TABLE0 + 2 * ROW
 AT_RAW0 = AT_PAGE2 + ROW // 2
-AT_PAGE3 = AT_PAGE2 + ROW
-AT_RAW1 = AT_PAGE3 + ROW
+AT_RAW1 = AT_RAW0 + ROW
 AT_TABLE1 = AT_RAW1 + ROW
 AT_PICKED = AT_TABLE1 + 2 * ROW
-AT_SCALES = AT_PICKED + ROW
+AT_SCALES = AT_PICKED + ROW + 64
 AT_GAIN = AT_SCALES + 2 * H
-AT_ROUNDED = AT_GAIN + 4 * H
+AT_ROUNDED = AT_GAIN + 4 * H + 4 * S
+FIRST = 256
 
 
 def tile_list_station_grid_increments_kernel(
@@ -57,18 +57,21 @@ def tile_list_station_grid_increments_kernel(
         z_sc = keep.tile([P, T2], U8, name="z_sc", align_bytes=64)
 
         table = [tenant([P, T], I32, "table0", AT_TABLE0), tenant([P, T], I32, "table1", AT_TABLE1)]
-        bias = tenant([P, PACK], F32, "bias", AT_ROUNDED)
-        base_rows = [tenant([P, T2], F32, "base%d" % t, (AT_TABLE1, AT_PICKED)[t % 2]) for t in range(PACK)]
+        bias = tenant([P, PACK], F32, "bias", AT_ROUNDED + 64)
+        base_at = (AT_PICKED + 64, AT_PICKED + 64 - ROW)
+        base_rows = [tenant([P, T2], F32, "base%d" % t, base_at[t % 2]) for t in range(PACK)]
         w_raw = [tenant([P, PACK * H], F32, "w_raw%d" % a, (AT_RAW0, AT_RAW1)[a]) for a in range(PASSES)]
-        page_at = (AT_TABLE0 + ROW, AT_PAGE2, AT_PAGE3)
+        page_at = (AT_TABLE0 + ROW, AT_PAGE2)
         page = [keep.tile([P, T2], F32, name="page0")]
-        page.extend(tenant([P, T2], F32, "page%d" % t, page_at[t - 1]) for t in range(1, PACK))
-        trust_at = (AT_ROUNDED + 64, AT_RAW1, AT_RAW1 + 4 * S, AT_TABLE1 + ROW)
-        trust = [tenant([P, S], F32, "trust%d" % t, trust_at[t]) for t in range(PACK)]
-        w_bf = [
-            tenant([P, PACK * H], BF16, "w_bf0", AT_ROUNDED),
-            keep.tile([P, PACK * H], BF16, name="w_bf1", align_bytes=64),
-        ]
+        page.extend(tenant([P, T2], F32, "page%d" % t, page_at[t - 1]) for t in range(1, PACK - 1))
+        page.append(page[0])
+        rest = S - FIRST
+        trust_first = tenant([P, 2, FIRST], F32, "trust_first", AT_ROUNDED + 128)
+        rest_at = (AT_ROUNDED + 64 - 4 * rest, AT_ROUNDED + 128 + 8 * FIRST)
+        trust_rest = [tenant([P, rest], F32, "trust_rest%d" % t, rest_at[t]) for t in range(2)]
+        trust_late = [tenant([P, S], F32, "trust%d" % t, AT_RAW1 + 4 * S * (t - 2)) for t in range(2, PACK)]
+        w_bf0 = tenant([P, PACK * H], BF16, "w_bf0", AT_ROUNDED)
+        w_bf1 = [keep.tile([P, 2 * H], BF16, name="w_bf1_%d" % v, align_bytes=64) for v in range(2)]
         table_sc = tenant([P, T // 4], I32, "table_sc", AT_TABLE1 - T // 2)
         picked_rows = keep.tile([P, S], U8, name="picked_rows", align_bytes=64)
         picked = [keep.tile([P, S], U32, name="picked0", align_bytes=64), tenant([P, S], U32, "picked1", AT_PICKED)]
@@ -76,28 +79,29 @@ def tile_list_station_grid_increments_kernel(
         w_sc = [keep.tile([P, H], U8, name="w_sc0", align_bytes=64), tenant([P, H], U8, "w_sc1", AT_SCALES)]
         gain = tenant([P, 2 * N], U8, "gain", AT_GAIN)
         limit = tenant([P, GROUPS], F32, "limit", AT_GAIN + 2 * N)
-        gain_sc = tenant([P, N // 4], I32, "gain_sc", AT_SCALES)
+        gain_sc = tenant([P, N // 4], I32, "gain_sc", rest_at[1])
 
         halves = [slice(u * HALF, (u + 1) * HALF) for u in range(2)]
-        list_halves = [slice(u * HALF // 16, (u + 1) * HALF // 16) for u in range(2)]
 
         def load_table(a):
             nc.sync.dma_start(table[a][:], tab_words[a].rearrange("p n i -> p (n i)").bitcast(I32))
 
-        def load_trust(t, cols):
-            src = wgs.rearrange("(s t) j -> t s j", t=PACK)[t]
+        def load_trust(tile, src):
             for q in (0, 2, 1, 3):
-                nc.sync.dma_start(trust[t][32 * q : 32 * (q + 1), cols], src[:, cols])
+                nc.sync.dma_start(tile[32 * q : 32 * (q + 1)], src)
 
         def load_base(t):
             nc.sync.dma_start(base_rows[t][:], base.rearrange("(p t) c -> t p c", t=PACK)[t])
 
-        def round_w1(a):
-            nc.scalar.copy(
-                w_bf[a][:].rearrange("p (t m j) -> p m t j", t=PACK, j=PACK),
-                w_raw[a][:].rearrange("p (j m t) -> p m t j", j=PACK, t=PACK),
+        def round_w1(copy, rounded, a, planes):
+            copy(
+                rounded[:].rearrange("p (t m j) -> p m t j", m=P, j=PACK),
+                w_raw[a][:].rearrange("p (j m t) -> p m t j", j=PACK, t=PACK)[:, :, planes, :],
             )
-            nc.vector.quantize_mx(out=w_codes[a][:].bitcast(FP8X4), scales=w_sc[a][:], in_=w_bf[a][:])
+
+        def quantise_w1(a, planes, rounded):
+            cols = slice(planes.start * P, planes.stop * P)
+            nc.vector.quantize_mx(out=w_codes[a][:, cols].bitcast(FP8X4), scales=w_sc[a][:, cols], in_=rounded)
 
         def load_w1(a):
             rows = w1[a * P * PACK : (a + 1) * P * PACK, :]
@@ -105,63 +109,83 @@ def tile_list_station_grid_increments_kernel(
 
         def place_scales(a):
             for q in range(4):
-                src = picked_rows[:].bitcast(I32)[16 * a + 4 * q : 16 * a + 4 * (q + 1), :]
+                src = picked_rows[:].bitcast(I32)[96 + 16 * a + 4 * q : 96 + 16 * a + 4 * (q + 1), :]
                 nc.sync.dma_start(picked_sc[a][32 * q : 32 * q + 4, :], src)
 
-        nc.sync.dma_start(table_sc[0:32, :], tab_scales.rearrange("a q n -> (a q) n").bitcast(I32))
+        nc.sync.dma_start(table_sc[96:P, :], tab_scales.rearrange("a q n -> (a q) n").bitcast(I32))
         nc.sync.dma_start(pick[:], offs)
         load_w1(0)
         load_table(0)
         nc.sync.dma_start(place[:], offs2)
-        nc.vector.memset(table_sc[64:P, :], 0)
-        nc.vector.memset(table_sc[32:64, :], 0)
+        nc.vector.memset(table_sc[0:96, :], 0)
         for a in range(PASSES):
             nc.vector.memset(picked_sc[a][:], 0)
 
         nc.vector.tensor_copy(picked_rows[:], table_sc[:].bitcast(U8).indirect(pick[:]))
         place_scales(0)
-        load_w1(1)
         load_table(1)
         place_scales(1)
+        load_w1(1)
+        round_w1(nc.scalar.copy, w_bf0, 0, slice(0, PACK))
         nc.vector.tensor_copy(picked[0][:], table[0][:].bitcast(U32).indirect(pick[:]))
-        for a in range(PASSES):
-            round_w1(a)
-        for t in range(PACK):
+        quantise_w1(0, slice(0, PACK), w_bf0[:])
+        for t in range(PACK - 1):
             nc.vector.memset(page[t][:], 0.0)
+        by_plane = wgs.rearrange("(s t) j -> s t j", t=PACK)
+        load_trust(trust_first, by_plane[:, 0:2, 0:FIRST])
         nc.sync.dma_start(bias[:], b1.rearrange("(p t) -> p t", t=PACK))
-        load_trust(0, halves[0])
-        load_trust(0, halves[1])
-        load_trust(1, slice(0, S))
-        load_trust(2, slice(0, S))
+        for t in range(2):
+            load_trust(trust_rest[t], by_plane[:, t, FIRST:S])
 
-        def first_product(acc, a, t, u):
+        def first_product(acc, a, t, cols):
             rows = slice(t * P, (t + 1) * P)
             nc.tensor.matmul_mx(
                 out=acc[:],
                 lhsT=w_codes[a][:, rows].bitcast(FP8X4),
                 lhsT_scale=w_sc[a][:, rows],
-                rhs=picked[a][:, halves[u]].bitcast(FP8X4),
-                rhs_scale=picked_sc[a][:].bitcast(U8)[:, halves[u]],
+                rhs=picked[a][:, cols].bitcast(FP8X4),
+                rhs_scale=picked_sc[a][:].bitcast(U8)[:, cols],
                 start=(a == 0),
                 stop=(a == PASSES - 1),
             )
 
-        h_acc = {}
-        for t in range(PACK):
-            for u in range(2):
-                h_acc[t, u] = psum.tile([P, HALF], F32, name="acc")
-                first_product(h_acc[t, u], 0, t, u)
+        lead, middle = slice(0, FIRST), slice(FIRST, HALF)
+        pieces_h = [(0, lead), (1, lead), (0, middle), (0, halves[1]), (1, middle), (1, halves[1])]
+        pieces_h.extend((t, cols) for t in range(2, PACK) for cols in halves)
+        h_acc = []
+        for t, cols in pieces_h[:8]:
+            h_acc.append(psum.tile([P, cols.stop - cols.start], F32, name="acc"))
+            first_product(h_acc[-1], 0, t, cols)
 
-        for u in range(2):
-            nc.vector.tensor_copy(
-                picked[1][:, halves[u]], table[1][:].bitcast(U32).indirect(pick[:, list_halves[u]])
-            )
-        for t in range(PACK):
-            for u in range(2):
-                first_product(h_acc[t, u], 1, t, u)
+        nc.vector.tensor_copy(picked[1][:], table[1][:].bitcast(U32).indirect(pick[:]))
+        round_w1(nc.vector.tensor_copy, w_bf1[0], 1, slice(0, 2))
+        round_w1(nc.scalar.copy, w_bf1[1], 1, slice(2, PACK))
+        for t in range(2):
+            quantise_w1(1, slice(t, t + 1), w_bf1[0][:, t * H : (t + 1) * H])
+        quantise_w1(1, slice(2, PACK), w_bf1[1][:])
+        for t in range(2, PACK):
+            load_trust(trust_late[t - 2], by_plane[:, t, :])
+
+        for i, (t, cols) in enumerate(pieces_h):
+            if i >= 8:
+                h_acc.append(psum.tile([P, cols.stop - cols.start], F32, name="acc"))
+                first_product(h_acc[i], 0, t, cols)
+            first_product(h_acc[i], 1, t, cols)
+            if i == 0:
+                nc.vector.scalar_tensor_tensor(
+                    anomaly[0][:, cols], h_acc[0][:], bias[:, 0:1], trust_first[:, 0, :], ALU.add, ALU.mult
+                )
+                continue
+            nc.scalar.activation(anomaly[t][:, cols], h_acc[i][:], ACT.Identity, bias=bias[:, t : t + 1])
+            if t >= 2:
+                weights = trust_late[t - 2][:, cols]
+            elif cols == lead:
+                weights = trust_first[:, t, :]
+            else:
+                weights = trust_rest[t][:, cols.start - FIRST : cols.stop - FIRST]
+            nc.gpsimd.tensor_tensor(anomaly[t][:, cols], anomaly[t][:, cols], weights, ALU.mult)
 
         load_base(0)
-        load_trust(3, slice(0, S))
         load_base(1)
         nc.gpsimd.memset(gain_sc[:], 0)
         nc.sync.dma_start(gain[:].bitcast(I32), gain_words[0].bitcast(I32))
@@ -170,12 +194,6 @@ def tile_list_station_grid_increments_kernel(
             nc.sync.dma_start(gain_sc[r:P:32, :], src.bitcast(I32))
         with nc.allow_non_contiguous_dma(reason="one value for each partition and output group"):
             nc.sync.dma_start(limit[:], lim.rearrange("(g p) -> p g", p=P))
-
-        def add_bias(t, u):
-            nc.scalar.activation(anomaly[t][:, halves[u]], h_acc[t, u][:], ACT.Identity, bias=bias[:, t : t + 1])
-
-        def weigh(t, cols):
-            nc.gpsimd.tensor_tensor(anomaly[t][:, cols], anomaly[t][:, cols], trust[t][:, cols], ALU.mult)
 
         def subtract(engine, t, cols):
             engine.tensor_tensor(z_rows[:, t, cols], page[t][:, cols], base_rows[t][:, cols], ALU.subtract)
@@ -186,23 +204,20 @@ def tile_list_station_grid_increments_kernel(
                 z_rows[:, first : first + 2, cols].rearrange("p t c -> p c t"),
             )
 
-        nc.vector.scalar_tensor_tensor(
-            anomaly[0][:, halves[0]], h_acc[0, 0][:], bias[:, 0:1], trust[0][:, halves[0]], ALU.add, ALU.mult
-        )
-        add_bias(0, 1)
-        weigh(0, halves[1])
-        for t in range(1, PACK):
-            for u in range(2):
-                add_bias(t, u)
-            weigh(t, slice(0, S))
-        for u in range(2):
-            nc.vector.tensor_copy(page[0][:].indirect(place[:, list_halves[u]]), anomaly[0][:, halves[u]])
-        for t in range(1, PACK):
-            nc.vector.tensor_copy(page[t][:].indirect(place[:]), anomaly[t][:])
+        def scatter(t, cols):
+            offsets = place[:, cols.start // 16 : cols.stop // 16]
+            nc.vector.tensor_copy(page[t][:].indirect(offsets), anomaly[t][:, cols])
+
+        for cols in (lead, slice(FIRST, S)):
+            for t in range(2):
+                scatter(t, cols)
+        scatter(2, slice(0, S))
         for t in range(PACK - 1):
             pieces = 1 if t == 0 else 2
             for v in range(pieces):
                 subtract(nc.gpsimd, t, slice(v * T2 // pieces, (v + 1) * T2 // pieces))
+            if t == 0:
+                scatter(PACK - 1, slice(0, S))
             if t + 2 < PACK:
                 load_base(t + 2)
 

@@ -57,7 +57,7 @@ def tile_list_station_grid_increments_kernel(
         z_sc = keep.tile([P, T2], U8, name="z_sc", align_bytes=64)
 
         table = [tenant([P, T], I32, "table0", AT_TABLE0), tenant([P, T], I32, "table1", AT_TABLE1)]
-        bias = tenant([P, PACK], F32, "bias", AT_ROUNDED + 64)
+        bias = keep.tile([P, PACK], F32, name="bias")
         base_at = (AT_PICKED + 64, AT_PICKED + 64 - ROW)
         base_rows = [tenant([P, T2], F32, "base%d" % t, base_at[t % 2]) for t in range(PACK)]
         w_raw = [tenant([P, PACK * H], F32, "w_raw%d" % a, (AT_RAW0, AT_RAW1)[a]) for a in range(PASSES)]
@@ -66,7 +66,7 @@ def tile_list_station_grid_increments_kernel(
         page.extend(tenant([P, T2], F32, "page%d" % t, page_at[t - 1]) for t in range(1, PACK - 1))
         page.append(page[0])
         rest = S - FIRST
-        trust_first = tenant([P, 2, FIRST], F32, "trust_first", AT_ROUNDED + 128)
+        trust_first = [tenant([P, FIRST], F32, "trust_first%d" % t, AT_ROUNDED + 128 + 4 * FIRST * t) for t in range(2)]
         rest_at = (AT_ROUNDED + 64 - 4 * rest, AT_ROUNDED + 128 + 8 * FIRST)
         trust_rest = [tenant([P, rest], F32, "trust_rest%d" % t, rest_at[t]) for t in range(2)]
         trust_late = [tenant([P, S], F32, "trust%d" % t, AT_RAW1 + 4 * S * (t - 2)) for t in range(2, PACK)]
@@ -108,15 +108,16 @@ def tile_list_station_grid_increments_kernel(
             nc.sync.dma_start(w_raw[a][:], rows.rearrange("(p j) c -> p (j c)", j=PACK))
 
         def place_scales(a):
-            for q in range(4):
-                src = picked_rows[:].bitcast(I32)[96 + 16 * a + 4 * q : 96 + 16 * a + 4 * (q + 1), :]
-                nc.sync.dma_start(picked_sc[a][32 * q : 32 * q + 4, :], src)
+            for r in range(4):
+                src = picked_rows[:].bitcast(I32)[96 + 16 * a + r : 96 + 16 * (a + 1) : 4, :]
+                nc.sync.dma_start(picked_sc[a][r:P:32, :], src)
 
         nc.sync.dma_start(table_sc[96:P, :], tab_scales.rearrange("a q n -> (a q) n").bitcast(I32))
         nc.sync.dma_start(pick[:], offs)
         load_w1(0)
         load_table(0)
         nc.sync.dma_start(place[:], offs2)
+        nc.sync.dma_start(bias[:], b1.rearrange("(p t) -> p t", t=PACK))
         nc.vector.memset(table_sc[0:96, :], 0)
         for a in range(PASSES):
             nc.vector.memset(picked_sc[a][:], 0)
@@ -124,16 +125,16 @@ def tile_list_station_grid_increments_kernel(
         nc.vector.tensor_copy(picked_rows[:], table_sc[:].bitcast(U8).indirect(pick[:]))
         place_scales(0)
         load_table(1)
-        place_scales(1)
         load_w1(1)
+        place_scales(1)
         round_w1(nc.scalar.copy, w_bf0, 0, slice(0, PACK))
         nc.vector.tensor_copy(picked[0][:], table[0][:].bitcast(U32).indirect(pick[:]))
         quantise_w1(0, slice(0, PACK), w_bf0[:])
         for t in range(PACK - 1):
             nc.vector.memset(page[t][:], 0.0)
         by_plane = wgs.rearrange("(s t) j -> s t j", t=PACK)
-        load_trust(trust_first, by_plane[:, 0:2, 0:FIRST])
-        nc.sync.dma_start(bias[:], b1.rearrange("(p t) -> p t", t=PACK))
+        for t in range(2):
+            load_trust(trust_first[t], by_plane[:, t, 0:FIRST])
         for t in range(2):
             load_trust(trust_rest[t], by_plane[:, t, FIRST:S])
 
@@ -173,14 +174,14 @@ def tile_list_station_grid_increments_kernel(
             first_product(h_acc[i], 1, t, cols)
             if i == 0:
                 nc.vector.scalar_tensor_tensor(
-                    anomaly[0][:, cols], h_acc[0][:], bias[:, 0:1], trust_first[:, 0, :], ALU.add, ALU.mult
+                    anomaly[0][:, cols], h_acc[0][:], bias[:, 0:1], trust_first[0][:], ALU.add, ALU.mult
                 )
                 continue
             nc.scalar.activation(anomaly[t][:, cols], h_acc[i][:], ACT.Identity, bias=bias[:, t : t + 1])
             if t >= 2:
                 weights = trust_late[t - 2][:, cols]
             elif cols == lead:
-                weights = trust_first[:, t, :]
+                weights = trust_first[t][:]
             else:
                 weights = trust_rest[t][:, cols.start - FIRST : cols.stop - FIRST]
             nc.gpsimd.tensor_tensor(anomaly[t][:, cols], anomaly[t][:, cols], weights, ALU.mult)

@@ -20,7 +20,7 @@ PACK = 4
 PASSES = K // (P * PACK)
 HALF = S // 2
 GROUPS = N // P
-CHUNKS = (256, 256, 512, 512, 512)
+CHUNKS = (128, 256, 256, 384, 512, 512)
 ROW = 4 * T2
 AT_TABLE0 = 0
 AT_PAGE2 = AT_TABLE0 + 2 * ROW
@@ -227,28 +227,35 @@ def tile_list_station_grid_increments_kernel(
         for cols in spans:
             pair_up(nc.scalar.copy, 0, cols)
 
+        def parts(cols):
+            if cols.stop - cols.start == 384:
+                return [slice(cols.start, cols.start + 128), slice(cols.start + 128, cols.stop)]
+            return [cols]
+
         def quantise_z(cols):
             subtract(nc.vector, PACK - 1, cols)
             pair_up(nc.scalar.copy if cols == spans[1] else nc.vector.tensor_copy, 2, cols)
-            nc.vector.quantize_mx(
-                out=z_codes[:, cols].bitcast(FP8X4),
-                scales=z_sc[:, cols],
-                in_=z_packed[:, cols, :].rearrange("p c t -> p (c t)"),
-            )
+            for part in parts(cols):
+                nc.vector.quantize_mx(
+                    out=z_codes[:, part].bitcast(FP8X4),
+                    scales=z_sc[:, part],
+                    in_=z_packed[:, part, :].rearrange("p c t -> p (c t)"),
+                )
 
         def increments(cols):
             width = cols.stop - cols.start
             for g in range(GROUPS):
                 acc = psum.tile([P, width], F32, name="acc")
-                nc.tensor.matmul_mx(
-                    out=acc[:],
-                    lhsT=gain[:, 2 * P * g : 2 * P * (g + 1)].bitcast(FP4X4),
-                    lhsT_scale=gain_sc[:].bitcast(U8)[:, P * g : P * (g + 1)],
-                    rhs=z_codes[:, cols].bitcast(FP8X4),
-                    rhs_scale=z_sc[:, cols],
-                    start=True,
-                    stop=True,
-                )
+                for part in parts(cols):
+                    nc.tensor.matmul_mx(
+                        out=acc[:, part.start - cols.start : part.stop - cols.start],
+                        lhsT=gain[:, 2 * P * g : 2 * P * (g + 1)].bitcast(FP4X4),
+                        lhsT_scale=gain_sc[:].bitcast(U8)[:, P * g : P * (g + 1)],
+                        rhs=z_codes[:, part].bitcast(FP8X4),
+                        rhs_scale=z_sc[:, part],
+                        start=True,
+                        stop=True,
+                    )
                 pieces = 2 if (cols.stop, g) == (T2, GROUPS - 1) else 1
                 step = width // pieces
                 for lo in range(0, width, step):

@@ -20,7 +20,7 @@ PACK = 4
 PASSES = K // (P * PACK)
 HALF = S // 2
 GROUPS = N // P
-CHUNKS = (128, 256, 256, 384, 512, 512)
+CHUNKS = (128, 128) + (256,) * 7
 ROW = 4 * T2
 AT_TABLE0 = 0
 AT_PAGE2 = AT_TABLE0 + 2 * ROW
@@ -227,45 +227,40 @@ def tile_list_station_grid_increments_kernel(
         for cols in spans:
             pair_up(nc.scalar.copy, 0, cols)
 
-        def parts(cols):
-            if cols.stop - cols.start == 384:
-                return [slice(cols.start, cols.start + 128), slice(cols.start + 128, cols.stop)]
-            return [cols]
-
-        def quantise_z(cols):
+        def quantise_z(i):
+            cols = spans[i]
             subtract(nc.vector, PACK - 1, cols)
-            pair_up(nc.scalar.copy if cols == spans[1] else nc.vector.tensor_copy, 2, cols)
-            for part in parts(cols):
-                nc.vector.quantize_mx(
-                    out=z_codes[:, part].bitcast(FP8X4),
-                    scales=z_sc[:, part],
-                    in_=z_packed[:, part, :].rearrange("p c t -> p (c t)"),
+            pair_up(nc.scalar.copy if i in (1, 2) else nc.vector.tensor_copy, 2, cols)
+            nc.vector.quantize_mx(
+                out=z_codes[:, cols].bitcast(FP8X4),
+                scales=z_sc[:, cols],
+                in_=z_packed[:, cols, :].rearrange("p c t -> p (c t)"),
+            )
+
+        def increments(g, chunks):
+            lo, hi = spans[chunks[0]].start, spans[chunks[-1]].stop
+            acc = psum.tile([P, hi - lo], F32, name="acc")
+            for i in chunks:
+                nc.tensor.matmul_mx(
+                    out=acc[:, spans[i].start - lo : spans[i].stop - lo],
+                    lhsT=gain[:, 2 * P * g : 2 * P * (g + 1)].bitcast(FP4X4),
+                    lhsT_scale=gain_sc[:].bitcast(U8)[:, P * g : P * (g + 1)],
+                    rhs=z_codes[:, spans[i]].bitcast(FP8X4),
+                    rhs_scale=z_sc[:, spans[i]],
+                    start=True,
+                    stop=True,
                 )
+            result = res.tile([P, hi - lo], F32, name="result")
+            nc.scalar.activation(result[:], acc[:], ACT.Tanh)
+            nc.vector.tensor_scalar(result[:], result[:], limit[:, g : g + 1], None, ALU.mult)
+            nc.sync.dma_start(out[P * g : P * (g + 1), lo:hi], result[:])
 
-        def increments(cols):
-            width = cols.stop - cols.start
-            for g in range(GROUPS):
-                acc = psum.tile([P, width], F32, name="acc")
-                for part in parts(cols):
-                    nc.tensor.matmul_mx(
-                        out=acc[:, part.start - cols.start : part.stop - cols.start],
-                        lhsT=gain[:, 2 * P * g : 2 * P * (g + 1)].bitcast(FP4X4),
-                        lhsT_scale=gain_sc[:].bitcast(U8)[:, P * g : P * (g + 1)],
-                        rhs=z_codes[:, part].bitcast(FP8X4),
-                        rhs_scale=z_sc[:, part],
-                        start=True,
-                        stop=True,
-                    )
-                pieces = 2 if (cols.stop, g) == (T2, GROUPS - 1) else 1
-                step = width // pieces
-                for lo in range(0, width, step):
-                    result = res.tile([P, step], F32, name="result")
-                    nc.scalar.activation(result[:], acc[:, lo : lo + step], ACT.Tanh)
-                    nc.vector.tensor_scalar(result[:], result[:], limit[:, g : g + 1], None, ALU.mult)
-                    nc.sync.dma_start(out[P * g : P * (g + 1), cols.start + lo : cols.start + lo + step], result[:])
-
-        quantise_z(spans[0])
+        quantise_z(0)
         for i in range(len(spans)):
             if i + 1 < len(spans):
-                quantise_z(spans[i + 1])
-            increments(spans[i])
+                quantise_z(i + 1)
+            closing = range(GROUPS // 2) if i % 2 == 0 else range(GROUPS // 2, GROUPS)
+            for g in closing:
+                increments(g, [c for c in (i - 1, i) if c >= 0])
+        for g in range(GROUPS // 2, GROUPS):
+            increments(g, [len(spans) - 1])

@@ -25,7 +25,8 @@ ROW = 4 * T2
 AT_TABLE0 = 0
 AT_PAGE2 = AT_TABLE0 + 2 * ROW
 AT_RAW0 = AT_PAGE2 + ROW // 2
-AT_RAW1 = AT_RAW0 + ROW
+AT_PAGE1 = AT_RAW0 + ROW
+AT_RAW1 = AT_PAGE1 + ROW
 AT_TABLE1 = AT_RAW1 + ROW
 AT_PICKED = AT_TABLE1 + 2 * ROW
 AT_SCALES = AT_PICKED + ROW + 64
@@ -41,7 +42,7 @@ def tile_list_station_grid_increments_kernel(
     with ExitStack() as ctx:
         keep = ctx.enter_context(tc.tile_pool(name="keep", bufs=1))
         turns = ctx.enter_context(tc.tile_pool(name="turns", bufs=1))
-        res = ctx.enter_context(tc.tile_pool(name="res", bufs=31))
+        res = ctx.enter_context(tc.tile_pool(name="res", bufs=30))
         psum = ctx.enter_context(tc.psum_pool(name="psum", bufs=8))
 
         def tenant(shape, dtype, name, offset):
@@ -61,7 +62,7 @@ def tile_list_station_grid_increments_kernel(
         base_at = (AT_PICKED + 64, AT_PICKED + 64 - ROW)
         base_rows = [tenant([P, T2], F32, "base%d" % t, base_at[t % 2]) for t in range(PACK)]
         w_raw = [tenant([P, PACK * H], F32, "w_raw%d" % a, (AT_RAW0, AT_RAW1)[a]) for a in range(PASSES)]
-        page_at = (AT_TABLE0 + ROW, AT_PAGE2)
+        page_at = (AT_PAGE1, AT_PAGE2)
         page = [keep.tile([P, T2], F32, name="page0")]
         page.extend(tenant([P, T2], F32, "page%d" % t, page_at[t - 1]) for t in range(1, PACK - 1))
         page.append(page[0])
@@ -72,7 +73,7 @@ def tile_list_station_grid_increments_kernel(
         trust_late = [tenant([P, S], F32, "trust%d" % t, AT_RAW1 + 4 * S * (t - 2)) for t in range(2, PACK)]
         w_bf0 = tenant([P, PACK * H], BF16, "w_bf0", AT_ROUNDED)
         w_bf1 = [keep.tile([P, 2 * H], BF16, name="w_bf1_%d" % v, align_bytes=64) for v in range(2)]
-        table_sc = tenant([P, T // 4], I32, "table_sc", AT_TABLE1 - T // 2)
+        table_sc = tenant([P, T // 4], I32, "table_sc", AT_RAW1 - T // 2)
         picked_rows = keep.tile([P, S], U8, name="picked_rows", align_bytes=64)
         picked = [keep.tile([P, S], U32, name="picked0", align_bytes=64), tenant([P, S], U32, "picked1", AT_PICKED)]
         w_codes = [keep.tile([P, H], U32, name="w_codes0", align_bytes=64), tenant([P, H], U32, "w_codes1", AT_GAIN)]
@@ -116,6 +117,7 @@ def tile_list_station_grid_increments_kernel(
         nc.sync.dma_start(pick[:], offs)
         load_w1(0)
         load_table(0)
+        load_table(1)
         nc.sync.dma_start(place[:], offs2)
         nc.sync.dma_start(bias[:], b1.rearrange("(p t) -> p t", t=PACK))
         nc.vector.memset(table_sc[0:96, :], 0)
@@ -124,7 +126,6 @@ def tile_list_station_grid_increments_kernel(
 
         nc.vector.tensor_copy(picked_rows[:], table_sc[:].bitcast(U8).indirect(pick[:]))
         place_scales(0)
-        load_table(1)
         load_w1(1)
         place_scales(1)
         round_w1(nc.scalar.copy, w_bf0, 0, slice(0, PACK))
@@ -154,7 +155,7 @@ def tile_list_station_grid_increments_kernel(
         pieces_h = [(0, lead), (1, lead), (0, middle), (0, halves[1]), (1, middle), (1, halves[1])]
         pieces_h.extend((t, cols) for t in range(2, PACK) for cols in halves)
         h_acc = []
-        for t, cols in pieces_h[:8]:
+        for t, cols in pieces_h[:6]:
             h_acc.append(psum.tile([P, cols.stop - cols.start], F32, name="acc"))
             first_product(h_acc[-1], 0, t, cols)
 
@@ -168,7 +169,7 @@ def tile_list_station_grid_increments_kernel(
             load_trust(trust_late[t - 2], by_plane[:, t, :])
 
         for i, (t, cols) in enumerate(pieces_h):
-            if i >= 8:
+            if i >= 6:
                 h_acc.append(psum.tile([P, cols.stop - cols.start], F32, name="acc"))
                 first_product(h_acc[i], 0, t, cols)
             first_product(h_acc[i], 1, t, cols)

@@ -31,7 +31,7 @@ AT_TABLE1 = AT_RAW1 + ROW
 AT_PICKED = AT_TABLE1 + 2 * ROW
 AT_SCALES = AT_PICKED + ROW + 64
 AT_GAIN = AT_SCALES + 2 * H
-AT_ROUNDED = AT_GAIN + 4 * H + 4 * S
+AT_ROUNDED = AT_GAIN + 4 * H + 8 * S
 FIRST = 256
 
 
@@ -70,7 +70,7 @@ def tile_list_station_grid_increments_kernel(
         trust_first = [tenant([P, FIRST], F32, "trust_first%d" % t, AT_ROUNDED + 128 + 4 * FIRST * t) for t in range(2)]
         rest_at = (AT_ROUNDED + 64 - 4 * rest, AT_ROUNDED + 128 + 8 * FIRST)
         trust_rest = [tenant([P, rest], F32, "trust_rest%d" % t, rest_at[t]) for t in range(2)]
-        trust_late = [tenant([P, S], F32, "trust%d" % t, AT_RAW1 + 4 * S * (t - 2)) for t in range(2, PACK)]
+        trust_late = [tenant([P, S], F32, "trust2", AT_RAW1), tenant([P, S], F32, "trust3", AT_GAIN + 2 * N + 64)]
         w_bf0 = tenant([P, PACK * H], BF16, "w_bf0", AT_ROUNDED)
         w_bf1 = [keep.tile([P, 2 * H], BF16, name="w_bf1_%d" % v, align_bytes=64) for v in range(2)]
         table_sc = tenant([P, T // 4], I32, "table_sc", AT_RAW1 - T // 2)
@@ -108,8 +108,8 @@ def tile_list_station_grid_increments_kernel(
             rows = w1[a * P * PACK : (a + 1) * P * PACK, :]
             nc.sync.dma_start(w_raw[a][:], rows.rearrange("(p j) c -> p (j c)", j=PACK))
 
-        def place_scales(a):
-            for r in range(4):
+        def place_scales(a, rows):
+            for r in rows:
                 src = picked_rows[:].bitcast(I32)[96 + 16 * a + r : 96 + 16 * (a + 1) : 4, :]
                 nc.sync.dma_start(picked_sc[a][r:P:32, :], src)
 
@@ -117,17 +117,18 @@ def tile_list_station_grid_increments_kernel(
         nc.sync.dma_start(pick[:], offs)
         load_w1(0)
         load_table(0)
+        nc.sync.dma_start(bias[:], b1.rearrange("(p t) -> p t", t=PACK))
         load_table(1)
         nc.sync.dma_start(place[:], offs2)
-        nc.sync.dma_start(bias[:], b1.rearrange("(p t) -> p t", t=PACK))
         nc.vector.memset(table_sc[0:96, :], 0)
         for a in range(PASSES):
             nc.vector.memset(picked_sc[a][:], 0)
 
         nc.vector.tensor_copy(picked_rows[:], table_sc[:].bitcast(U8).indirect(pick[:]))
-        place_scales(0)
+        place_scales(0, range(4))
+        place_scales(1, range(1))
         load_w1(1)
-        place_scales(1)
+        place_scales(1, range(1, 4))
         round_w1(nc.scalar.copy, w_bf0, 0, slice(0, PACK))
         nc.vector.tensor_copy(picked[0][:], table[0][:].bitcast(U32).indirect(pick[:]))
         quantise_w1(0, slice(0, PACK), w_bf0[:])
@@ -165,8 +166,7 @@ def tile_list_station_grid_increments_kernel(
         for t in range(2):
             quantise_w1(1, slice(t, t + 1), w_bf1[0][:, t * H : (t + 1) * H])
         quantise_w1(1, slice(2, PACK), w_bf1[1][:])
-        for t in range(2, PACK):
-            load_trust(trust_late[t - 2], by_plane[:, t, :])
+        load_trust(trust_late[0], by_plane[:, 2, :])
 
         for i, (t, cols) in enumerate(pieces_h):
             if i >= 6:
@@ -179,8 +179,10 @@ def tile_list_station_grid_increments_kernel(
                 )
                 continue
             nc.scalar.activation(anomaly[t][:, cols], h_acc[i][:], ACT.Identity, bias=bias[:, t : t + 1])
-            if t >= 2:
-                weights = trust_late[t - 2][:, cols]
+            if t == PACK - 1:
+                continue
+            if t == 2:
+                weights = trust_late[0][:, cols]
             elif cols == lead:
                 weights = trust_first[t][:]
             else:
@@ -188,6 +190,7 @@ def tile_list_station_grid_increments_kernel(
             nc.gpsimd.tensor_tensor(anomaly[t][:, cols], anomaly[t][:, cols], weights, ALU.mult)
 
         load_base(0)
+        load_trust(trust_late[1], by_plane[:, PACK - 1, :])
         load_base(1)
         nc.gpsimd.memset(gain_sc[:], 0)
         nc.sync.dma_start(gain[:].bitcast(I32), gain_words[0].bitcast(I32))
@@ -219,6 +222,7 @@ def tile_list_station_grid_increments_kernel(
             for v in range(pieces):
                 subtract(nc.gpsimd, t, slice(v * T2 // pieces, (v + 1) * T2 // pieces))
             if t == 0:
+                nc.gpsimd.tensor_tensor(anomaly[PACK - 1][:], anomaly[PACK - 1][:], trust_late[1][:], ALU.mult)
                 scatter(PACK - 1, slice(0, S))
             if t + 2 < PACK:
                 load_base(t + 2)

from contextlib import ExitStack

import concourse.mybir as mybir

K, T, S, T2, H, N, P = 1024, 4096, 1024, 2048, 512, 768, 128
FLOPS = 2 * K * H * S + 2 * H * N * T2

F32 = mybir.dt.float32
BF16 = mybir.dt.bfloat16
I32 = mybir.dt.int32
U32 = mybir.dt.uint32
U16 = mybir.dt.uint16
U8 = mybir.dt.uint8
FP8X4 = mybir.dt.float8_e4m3fn_x4
FP4X4 = mybir.dt.float4_e2m1fn_x4
ALU = mybir.AluOpType
ACT = mybir.ActivationFunctionType

PACK = 4
PASSES = K // (P * PACK)
HALF = S // 2
GROUPS = N // P
CHUNKS = (128, 128) + (256,) * 7
ROW = 4 * T2
AT_TABLE0 = 0
AT_PAGE2 = AT_TABLE0 + 2 * ROW
AT_RAW0 = AT_PAGE2 + ROW // 2
AT_PAGE1 = AT_RAW0 + ROW
AT_RAW1 = AT_PAGE1 + ROW
AT_TABLE1 = AT_RAW1 + ROW
AT_PICKED = AT_TABLE1 + 2 * ROW
AT_SCALES = AT_PICKED + ROW + 64
AT_GAIN = AT_SCALES + 2 * H
AT_ROUNDED = AT_GAIN + 4 * H + 8 * S
FIRST = 256


def tile_list_station_grid_increments_kernel(
    tc, tab_words, tab_scales, offs, w1, b1, wgs, offs2, base, gain_words, gain_scales, lim, out
):
    nc = tc.nc
    with ExitStack() as ctx:
        keep = ctx.enter_context(tc.tile_pool(name="keep", bufs=1))
        turns = ctx.enter_context(tc.tile_pool(name="turns", bufs=1))
        res = ctx.enter_context(tc.tile_pool(name="res", bufs=30))
        psum = ctx.enter_context(tc.psum_pool(name="psum", bufs=8))

        def tenant(shape, dtype, name, offset):
            return turns.tile(shape, dtype, name=name, align_bytes=64, offset=offset)

        pick = keep.tile([P, S // 16], U16, name="pick")
        place = keep.tile([P, S // 16], U16, name="place")
        picked_sc = [keep.tile([P, S // 4], I32, name="picked_sc%d" % a, align_bytes=64) for a in range(PASSES)]
        anomaly = [keep.tile([P, S], F32, name="anomaly%d" % t) for t in range(PACK)]
        z_rows = keep.tile([P, PACK, T2], BF16, name="z_rows", align_bytes=64)
        z_packed = keep.tile([P, T2, PACK], BF16, name="z_packed", align_bytes=64)
        z_codes = keep.tile([P, T2], U32, name="z_codes", align_bytes=64)
        z_sc = keep.tile([P, T2], U8, name="z_sc", align_bytes=64)

        table = [tenant([P, T], I32, "table0", AT_TABLE0), tenant([P, T], I32, "table1", AT_TABLE1)]
        bias = keep.tile([P, PACK], F32, name="bias")
        base_at = (AT_PICKED + 64, AT_PICKED + 64 - ROW)
        base_rows = [tenant([P, T2], F32, "base%d" % t, base_at[t % 2]) for t in range(PACK)]
        w_raw = [tenant([P, PACK * H], F32, "w_raw%d" % a, (AT_RAW0, AT_RAW1)[a]) for a in range(PASSES)]
        page_at = (AT_PAGE1, AT_PAGE2)
        page = [keep.tile([P, T2], F32, name="page0")]
        page.extend(tenant([P, T2], F32, "page%d" % t, page_at[t - 1]) for t in range(1, PACK - 1))
        page.append(page[0])
        rest = S - FIRST
        trust_first = [tenant([P, FIRST], F32, "trust_first%d" % t, AT_ROUNDED + 128 + 4 * FIRST * t) for t in range(2)]
        rest_at = (AT_ROUNDED + 64 - 4 * rest, AT_ROUNDED + 128 + 8 * FIRST)
        trust_rest = [tenant([P, rest], F32, "trust_rest%d" % t, rest_at[t]) for t in range(2)]
        trust_late = [tenant([P, S], F32, "trust2", AT_RAW1), tenant([P, S], F32, "trust3", AT_GAIN + 2 * N + 64)]
        w_bf0 = tenant([P, PACK * H], BF16, "w_bf0", AT_ROUNDED)
        w_bf1 = [keep.tile([P, 2 * H], BF16, name="w_bf1_%d" % v, align_bytes=64) for v in range(2)]
        table_sc = tenant([P, T // 4], I32, "table_sc", AT_RAW1 - T // 2)
        picked_rows = keep.tile([P, S], U8, name="picked_rows", align_bytes=64)
        picked = [keep.tile([P, S], U32, name="picked0", align_bytes=64), tenant([P, S], U32, "picked1", AT_PICKED)]
        w_codes = [keep.tile([P, H], U32, name="w_codes0", align_bytes=64), tenant([P, H], U32, "w_codes1", AT_GAIN)]
        w_sc = [keep.tile([P, H], U8, name="w_sc0", align_bytes=64), tenant([P, H], U8, "w_sc1", AT_SCALES)]
        gain = tenant([P, 2 * N], U8, "gain", AT_GAIN)
        limit = tenant([P, GROUPS], F32, "limit", AT_GAIN + 2 * N)
        gain_sc = tenant([P, N // 4], I32, "gain_sc", rest_at[1])

        halves = [slice(u * HALF, (u + 1) * HALF) for u in range(2)]

        def load_table(a):
            nc.sync.dma_start(table[a][:], tab_words[a].rearrange("p n i -> p (n i)").bitcast(I32))

        def load_trust(tile, src):
            for q in (0, 2, 1, 3):
                nc.sync.dma_start(tile[32 * q : 32 * (q + 1)], src)

        def load_base(t):
            nc.sync.dma_start(base_rows[t][:], base.rearrange("(p t) c -> t p c", t=PACK)[t])

        def round_w1(copy, rounded, a, planes):
            copy(
                rounded[:].rearrange("p (t m j) -> p m t j", m=P, j=PACK),
                w_raw[a][:].rearrange("p (j m t) -> p m t j", j=PACK, t=PACK)[:, :, planes, :],
            )

        def quantise_w1(a, planes, rounded):
            cols = slice(planes.start * P, planes.stop * P)
            nc.vector.quantize_mx(out=w_codes[a][:, cols].bitcast(FP8X4), scales=w_sc[a][:, cols], in_=rounded)

        def load_w1(a):
            rows = w1[a * P * PACK : (a + 1) * P * PACK, :]
            nc.sync.dma_start(w_raw[a][:], rows.rearrange("(p j) c -> p (j c)", j=PACK))

        def place_scales(a, rows):
            for r in rows:
                src = picked_rows[:].bitcast(I32)[96 + 16 * a + r : 96 + 16 * (a + 1) : 4, :]
                nc.sync.dma_start(picked_sc[a][r:P:32, :], src)

        nc.sync.dma_start(table_sc[96:P, :], tab_scales.rearrange("a q n -> (a q) n").bitcast(I32))
        nc.sync.dma_start(pick[:], offs)
        load_w1(0)
        load_table(0)
        nc.sync.dma_start(bias[:], b1.rearrange("(p t) -> p t", t=PACK))
        load_table(1)
        nc.sync.dma_start(place[:], offs2)
        nc.vector.memset(table_sc[0:96, :], 0)
        for a in range(PASSES):
            nc.vector.memset(picked_sc[a][:], 0)

        nc.vector.tensor_copy(picked_rows[:], table_sc[:].bitcast(U8).indirect(pick[:]))
        place_scales(0, range(4))
        place_scales(1, range(1))
        load_w1(1)
        place_scales(1, range(1, 4))
        round_w1(nc.scalar.copy, w_bf0, 0, slice(0, PACK))
        nc.vector.tensor_copy(picked[0][:], table[0][:].bitcast(U32).indirect(pick[:]))
        quantise_w1(0, slice(0, PACK), w_bf0[:])
        for t in range(PACK - 1):
            nc.vector.memset(page[t][:], 0.0)
        by_plane = wgs.rearrange("(s t) j -> s t j", t=PACK)
        for t in range(2):
            load_trust(trust_first[t], by_plane[:, t, 0:FIRST])
        for t in range(2):
            load_trust(trust_rest[t], by_plane[:, t, FIRST:S])

        def first_product(acc, a, t, cols):
            rows = slice(t * P, (t + 1) * P)
            nc.tensor.matmul_mx(
                out=acc[:],
                lhsT=w_codes[a][:, rows].bitcast(FP8X4),
                lhsT_scale=w_sc[a][:, rows],
                rhs=picked[a][:, cols].bitcast(FP8X4),
                rhs_scale=picked_sc[a][:].bitcast(U8)[:, cols],
                start=(a == 0),
                stop=(a == PASSES - 1),
            )

        lead, middle = slice(0, FIRST), slice(FIRST, HALF)
        pieces_h = [(0, lead), (1, lead), (0, middle), (0, halves[1]), (1, middle), (1, halves[1])]
        pieces_h.extend((t, cols) for t in range(2, PACK) for cols in halves)
        h_acc = []
        for t, cols in pieces_h[:6]:
            h_acc.append(psum.tile([P, cols.stop - cols.start], F32, name="acc"))
            first_product(h_acc[-1], 0, t, cols)

        nc.vector.tensor_copy(picked[1][:], table[1][:].bitcast(U32).indirect(pick[:]))
        round_w1(nc.vector.tensor_copy, w_bf1[0], 1, slice(0, 2))
        round_w1(nc.scalar.copy, w_bf1[1], 1, slice(2, PACK))
        for t in range(2):
            quantise_w1(1, slice(t, t + 1), w_bf1[0][:, t * H : (t + 1) * H])
        quantise_w1(1, slice(2, PACK), w_bf1[1][:])
        load_trust(trust_late[0], by_plane[:, 2, :])

        for i, (t, cols) in enumerate(pieces_h):
            if i >= 6:
                h_acc.append(psum.tile([P, cols.stop - cols.start], F32, name="acc"))
                first_product(h_acc[i], 0, t, cols)
            first_product(h_acc[i], 1, t, cols)
            if i == 0:
                nc.vector.scalar_tensor_tensor(
                    anomaly[0][:, cols], h_acc[0][:], bias[:, 0:1], trust_first[0][:], ALU.add, ALU.mult
                )
                continue
            nc.scalar.activation(anomaly[t][:, cols], h_acc[i][:], ACT.Identity, bias=bias[:, t : t + 1])
            if t == PACK - 1:
                continue
            if t == 2:
                weights = trust_late[0][:, cols]
            elif cols == lead:
                weights = trust_first[t][:]
            else:
                weights = trust_rest[t][:, cols.start - FIRST : cols.stop - FIRST]
            nc.gpsimd.tensor_tensor(anomaly[t][:, cols], anomaly[t][:, cols], weights, ALU.mult)

        load_base(0)
        load_trust(trust_late[1], by_plane[:, PACK - 1, :])
        load_base(1)
        nc.gpsimd.memset(gain_sc[:], 0)
        nc.sync.dma_start(gain[:].bitcast(I32), gain_words[0].bitcast(I32))
        for r in range(4):
            src = gain_scales[0].rearrange("(q r) n -> r q n", r=4)[r]
            nc.sync.dma_start(gain_sc[r:P:32, :], src.bitcast(I32))
        with nc.allow_non_contiguous_dma(reason="one value for each partition and output group"):
            nc.sync.dma_start(limit[:], lim.rearrange("(g p) -> p g", p=P))

        def subtract(engine, t, cols):
            engine.tensor_tensor(z_rows[:, t, cols], page[t][:, cols], base_rows[t][:, cols], ALU.subtract)

        def pair_up(copy, first, cols):
            copy(
                z_packed[:, cols, first : first + 2],
                z_rows[:, first : first + 2, cols].rearrange("p t c -> p c t"),
            )

        def scatter(t, cols):
            offsets = place[:, cols.start // 16 : cols.stop // 16]
            nc.vector.tensor_copy(page[t][:].indirect(offsets), anomaly[t][:, cols])

        for cols in (lead, slice(FIRST, S)):
            for t in range(2):
                scatter(t, cols)
        scatter(2, slice(0, S))
        for t in range(PACK - 1):
            pieces = 1 if t == 0 else 2
            for v in range(pieces):
                subtract(nc.gpsimd, t, slice(v * T2 // pieces, (v + 1) * T2 // pieces))
            if t == 0:
                nc.gpsimd.tensor_tensor(anomaly[PACK - 1][:], anomaly[PACK - 1][:], trust_late[1][:], ALU.mult)
                scatter(PACK - 1, slice(0, S))
            if t + 2 < PACK:
                load_base(t + 2)

        starts = [sum(CHUNKS[:i]) for i in range(len(CHUNKS))]
        spans = [slice(s, s + w) for s, w in zip(starts, CHUNKS)]
        for cols in spans:
            pair_up(nc.scalar.copy, 0, cols)

        def quantise_z(i):
            cols = spans[i]
            subtract(nc.vector, PACK - 1, cols)
            pair_up(nc.scalar.copy if i in (1, 2) else nc.vector.tensor_copy, 2, cols)
            nc.vector.quantize_mx(
                out=z_codes[:, cols].bitcast(FP8X4),
                scales=z_sc[:, cols],
                in_=z_packed[:, cols, :].rearrange("p c t -> p (c t)"),
            )

        def increments(g, chunks):
            lo, hi = spans[chunks[0]].start, spans[chunks[-1]].stop
            acc = psum.tile([P, hi - lo], F32, name="acc")
            for i in chunks:
                nc.tensor.matmul_mx(
                    out=acc[:, spans[i].start - lo : spans[i].stop - lo],
                    lhsT=gain[:, 2 * P * g : 2 * P * (g + 1)].bitcast(FP4X4),
                    lhsT_scale=gain_sc[:].bitcast(U8)[:, P * g : P * (g + 1)],
                    rhs=z_codes[:, spans[i]].bitcast(FP8X4),
                    rhs_scale=z_sc[:, spans[i]],
                    start=True,
                    stop=True,
                )
            result = res.tile([P, hi - lo], F32, name="result")
            nc.scalar.activation(result[:], acc[:], ACT.Tanh)
            nc.vector.tensor_scalar(result[:], result[:], limit[:, g : g + 1], None, ALU.mult)
            nc.sync.dma_start(out[P * g : P * (g + 1), lo:hi], result[:])

        quantise_z(0)
        for i in range(len(spans)):
            if i + 1 < len(spans):
                quantise_z(i + 1)
            closing = range(GROUPS // 2) if i % 2 == 0 else range(GROUPS // 2, GROUPS)
            for g in closing:
                increments(g, [c for c in (i - 1, i) if c >= 0])
        for g in range(GROUPS // 2, GROUPS):
            increments(g, [len(spans) - 1])
